import numpy as np
import ml_dtypes


def mxq(x, axis, fmt="e4m3"):
    dtype, down = {"e4m3": (ml_dtypes.float8_e4m3fn, 7), "e5m2": (ml_dtypes.float8_e5m2, 14)}[fmt]
    v = np.moveaxis(np.asarray(x, np.float32).astype(ml_dtypes.bfloat16).astype(np.float64), axis, -1)
    blocks = v.reshape(v.shape[:-1] + (-1, 32))
    amax = np.abs(blocks).max(-1, keepdims=True)
    byte = np.maximum(np.where(amax > 0, np.frexp(amax)[1] - 1 + 127, 0) - down, 1)
    scale = np.exp2(byte - 127.0)
    codes = (blocks / scale).astype(np.float32).astype(dtype).astype(np.float64)
    return np.moveaxis((codes * scale).reshape(v.shape), -1, axis)


WIDE = False


def mx_kscale(k):
    if not WIDE:
        return np.ones(k)
    levels = np.array([10, -10, 5, -5, 0])
    if k % 512:
        return np.exp2(np.random.permutation(np.resize(levels, k // 32))).repeat(32)
    a = np.empty((k // 512, 16))
    for p in range(k // 512):
        a[p, :8] = np.random.permutation(np.resize(levels, 8))
        for g in range(8):
            far = levels[np.abs(levels - a[p, g]) >= 10]
            a[p, g + 8] = far[np.random.randint(len(far))]
    return np.exp2(a.ravel()).repeat(32)


BF16 = ml_dtypes.bfloat16


def bf(x):
    return np.asarray(x, np.float32).astype(BF16)


def f64(x):
    return np.asarray(x).astype(np.float64)


E2M1 = np.array([0.0, 0.5, 1.0, 1.5, 2.0, 3.0, 4.0, 6.0, -0.0, -0.5, -1.0, -1.5, -2.0, -3.0, -4.0, -6.0])


def pack_weight(w, fmt):
    k, n = w.shape
    w = f64(bf(w)).reshape(k // 32, 32, n)
    amax = np.abs(w).max(1)
    if fmt == "e4m3":
        byte = np.frexp(amax)[1] - 1 + 127 - 7
    else:
        mant, ex = np.frexp(amax / 6.0)
        byte = np.where(mant > 0.5, ex, ex - 1) + 127
    byte = np.clip(np.where(amax > 0, byte, 1), 1, 254)
    scaled = (w * np.exp2(127.0 - byte)[:, None, :]).reshape(k, n).astype(np.float32)
    by_word = np.ascontiguousarray(scaled.reshape(k // 512, 128, 4, n).transpose(0, 1, 3, 2))
    if fmt == "e4m3":
        words = by_word.astype(ml_dtypes.float8_e4m3fn).view(np.uint8)
    else:
        c = by_word.astype(ml_dtypes.float4_e2m1fn).view(np.uint8) & 0xF
        words = c[..., 0::2] | (c[..., 1::2] << 4)
    return np.ascontiguousarray(words), np.ascontiguousarray(byte.astype(np.uint8).reshape(k // 512, 16, n))


def unpack_weight(words, scales, fmt):
    g, p, n, _ = words.shape
    if fmt == "e4m3":
        vals = np.ascontiguousarray(words).view(ml_dtypes.float8_e4m3fn).astype(np.float64)
    else:
        nib = np.empty((g, p, n, 4), np.uint8)
        nib[..., 0::2] = words & 0xF
        nib[..., 1::2] = words >> 4
        vals = E2M1[nib]
    vals = vals * np.repeat(np.exp2(scales.astype(np.float64) - 127.0), 8, axis=1)[..., None]
    return vals.transpose(0, 1, 3, 2).reshape(g * 512, n)
def pack4(w):
    words, scales = pack_weight(w, "e2m1")
    return words.reshape(words.shape[0], 128, -1), scales


def unpack4(words, scales):
    return unpack_weight(words.reshape(words.shape[0], 128, -1, 2), scales, "e2m1")


def planes(Y):
    n, m = Y.shape
    b = f64(bf(Y)).reshape(n // 32, 32, m)
    amax = np.abs(b).max(1)
    byte = np.clip(np.where(amax > 0, np.frexp(amax)[1] - 1 + 127 - 7, 1), 1, 254)
    codes = (b * np.exp2(127.0 - byte)[:, None, :]).reshape(n, m).astype(np.float32).astype(ml_dtypes.float8_e4m3fn).view(np.uint8)
    words = codes.reshape(n // 512, 128, 4, m).transpose(0, 1, 3, 2)
    return np.ascontiguousarray(words), np.ascontiguousarray(byte.astype(np.uint8).reshape(n // 512, 16, m))


N, K, V, F, T = 512, 1024, 2048, 512, 1024

def setup_inputs():
    rn = np.random.randn
    s, t, u = mx_kscale(K), mx_kscale(V), mx_kscale(F)
    f = np.random.uniform(0.1, 0.9, K)
    x = (np.random.binomial(2, f, (N, K)) - 2 * f) / np.sqrt(2 * f * (1 - f))
    h = rn(K, V) / np.sqrt(K)
    load = rn(F, V)
    fv = np.random.uniform(0.05, 0.5, V)
    impute_words, impute_scales = pack4(h / s[:, None])
    load_words, load_scales = pack_weight(load * u[:, None], "e4m3")
    return {
        "x": bf(x * s),
        "impute_words": impute_words, "impute_scales": impute_scales,
        "load_words": load_words, "load_scales": load_scales,
        "trait_factors": bf(rn(F, T) / np.sqrt(F) / u[:, None]),
        "dosage_scale": bf(np.sqrt(2 * fv * (1 - fv)) * t),
        "variant_weight": bf(np.random.uniform(0.2, 2.0, V) * 4 / np.sqrt(V) / t),
        "ancestry": bf(rn(N)),
        "slope": bf(rn(T)),
        "intercept": bf(0.5 * rn(T)),
        "trait_scale": bf(0.4 * np.exp(0.8 * rn(T))),
    }

def reference(x, impute_words, impute_scales, load_words, load_scales, trait_factors,
              dosage_scale, variant_weight, ancestry, slope, intercept, trait_scale):
    h = unpack4(impute_words, impute_scales)
    load = unpack_weight(load_words, load_scales, "e4m3")
    dosage = (mxq(f64(x), 1) @ h) * f64(dosage_scale)
    effect = (load.T @ mxq(f64(trait_factors), 0)) * f64(variant_weight)[:, None]
    score = mxq(dosage, 1) @ mxq(effect, 0)
    expected = f64(ancestry)[:, None] * f64(slope) + f64(intercept)
    y = (score - expected) * f64(trait_scale)
    words, scales = planes(y.T)
    return y, words, scales

@@ -1,0 +1,484 @@
+from contextlib import ExitStack
+
+import concourse.mybir as mybir
+from concourse.masks import make_identity
+
+N, K, V, F, T = 512, 1024, 2048, 512, 1024
+FLOPS = 2 * (N * K * V + V * F * T + N * V * T)
+
+F32 = mybir.dt.float32
+BF16 = mybir.dt.bfloat16
+I32 = mybir.dt.int32
+U8 = mybir.dt.uint8
+FP8X4 = mybir.dt.float8_e4m3fn_x4
+FP4X4 = mybir.dt.float4_e2m1fn_x4
+ALU = mybir.AluOpType
+ACT = mybir.ActivationFunctionType
+
+P = 128
+W = 512
+
+
+def tile_ancestry_adjusted_polygenic_scores_k4_kernel(
+    tc, x, impute_words, impute_scales, load_words, load_scales, trait_factors,
+    dosage_scale, variant_weight, ancestry, slope, intercept, trait_scale,
+    out_0, out_1, out_2,
+):
+    nc = tc.nc
+    with ExitStack() as ctx:
+        keep = ctx.enter_context(tc.tile_pool(name="keep", bufs=1))
+        flow = ctx.enter_context(tc.tile_pool(name="flow", bufs=1))
+        psum = ctx.enter_context(tc.psum_pool(name="psum", bufs=1))
+        ctx.enter_context(tc.manual_schedule(engines={mybir.EngineType.SP}))
+
+        def kept(name, shape, dtype):
+            return keep.tile(shape, dtype, name=name, align_bytes=64)
+
+        def rot_bank(name, shape):
+            return psum.tile(shape, F32, name=name, tag="rot", bufs=4)
+
+        def acc_bank(name, j, shape):
+            return psum.tile(shape, F32, name=name, tag="acc%d" % j, bufs=1)
+
+        h_words = impute_words.bitcast(I32)
+        h_scales = impute_scales.bitcast(I32)
+        l_words = load_words[0].rearrange("p n t -> p (n t)").bitcast(I32)
+        l_scales = load_scales[0].bitcast(I32)
+
+        ident = kept("ident", [P, P], F32)
+        x_raw = [kept("x_raw%d" % i, [P, 2, K], BF16) for i in range(2)]
+        h_raw = [kept("h_raw%d" % G, [P, 2, 256], I32) for G in range(4)]
+        l_raw = [kept("l_raw%d" % G, [P, W], I32) for G in range(4)]
+        c_raw = [[kept("c_raw%d%d" % (g, h), [P, 4, 256], BF16) for h in range(2)] for g in range(1)] + [kept("c_raw1", [P, 4, W], BF16)]
+        hs_raw = kept("hs_raw", [P, 2, W], I32)
+        ls_raw = kept("ls_raw", [P, P], I32)
+        v_rows = kept("v_rows", [4, W], BF16)
+        v_sorted = kept("v_sorted", [P, 4, P], F32)
+        v_cols = kept("v_cols", [P, 4, 4], F32)
+        d_rows = kept("d_rows", [4, W], BF16)
+        d_sorted = kept("d_sorted", [P, 4, P], F32)
+        d_cols = kept("d_cols", [P, 4, 4], F32)
+        t_rows = kept("t_rows", [7, W], BF16)
+        t_wide = kept("t_wide", [P, W], F32)
+        t_cols = kept("t_cols", [P, 7, 4], F32)
+        anc_all = kept("anc_all", [P, N], F32)
+        ab_col = kept("ab_col", [P, 2, 8], F32)
+        h_st = [kept("h_st%d" % G, [P, 2, 1024], U8) for G in range(4)]
+        hs_st = [kept("hs_st%d" % G, [P, 2, W], U8) for G in range(4)]
+        l_st = [kept("l_st%d" % G, [P, W], I32) for G in range(4)]
+        ls_st = kept("ls_st", [P, W], U8)
+        x_t = kept("x_t", [P, 2, N, 2], F32)
+        x_codes = [kept("x_codes%d" % g, [P, N], I32) for g in range(2)]
+        x_sc = [kept("x_sc%d" % g, [P, N], U8) for g in range(2)]
+        c_codes = [kept("c_codes%d" % g, [P, W], I32) for g in range(2)]
+        c_sc = [kept("c_sc%d" % g, [P, W], U8) for g in range(2)]
+        keys = [("D", G) for G in range(4)] + [("B", g, G) for g in range(2) for G in range(4)]
+        codes = {}
+        scales = {}
+        for key in keys:
+            label = "".join(str(s) for s in key)
+            codes[key] = [kept("codes%s_%d" % (label, h), [P, 256], I32) for h in range(2)] if key[0] == "B" else kept("codes%s" % label, [P, W], I32)
+            scales[key] = [kept("scales%s_%d" % (label, h), [P, 256], U8) for h in range(2)] if key[0] == "B" else kept("scales%s" % label, [P, W], U8)
+        y_t = [kept("y_t%d" % g, [P, 4, N], F32) for g in range(2)]
+        y_codes = [kept("y_codes%d" % g, [P, N], I32) for g in range(2)]
+        y_sc = kept("y_sc", [P, 2, N], U8)
+
+        make_identity(nc, ident[:])
+        nc.vector.memset(v_sorted[:], 0.0)
+        nc.vector.memset(ls_raw[:], 0)
+        nc.vector.memset(hs_raw[:], 0)
+        nc.vector.memset(d_sorted[:], 0.0)
+        nc.scalar.activation(out=t_wide[:], in_=v_sorted[:].rearrange("p t m -> p (t m)"), func=ACT.Copy)
+
+        def load_x(i):
+            nc.sync.dma_start(out=x_raw[i][:], in_=x[256 * i:256 * (i + 1), :].rearrange("(i p) k -> p i k", p=P))
+
+        def load_h(G):
+            nc.sync.dma_start(out=h_raw[G][:], in_=h_words[:, :, 256 * G:256 * (G + 1)].rearrange("g p c -> p g c"))
+
+        def load_l(G):
+            nc.sync.dma_start(out=l_raw[G][:], in_=l_words[:, W * G:W * (G + 1)])
+
+        def load_c(g):
+            nc.sync.dma_start(out=c_raw[g][:], in_=trait_factors[:, W * g:W * (g + 1)].rearrange("(p f) c -> p f c", f=4))
+
+        def load_c_half(h):
+            nc.sync.dma_start(out=c_raw[0][h][:], in_=trait_factors[:, 256 * h:256 * (h + 1)].rearrange("(p f) c -> p f c", f=4))
+
+        nc.sync.dma_start(out=v_rows[:], in_=variant_weight.rearrange("(G c) -> G c", G=4))
+        load_c_half(0)
+        load_l(0)
+        for Q in range(4):
+            nc.sync.dma_start(out=ls_raw[32 * Q:32 * Q + 16, :], in_=l_scales[4 * Q:4 * Q + 4, :].rearrange("r (G c) -> G r c", G=4))
+        load_c_half(1)
+        load_l(1)
+        nc.sync.dma_start(out=d_rows[:], in_=dosage_scale.rearrange("(G c) -> G c", G=4))
+        load_x(0)
+        load_x(1)
+        load_l(2)
+        for Q in range(4):
+            nc.sync.dma_start(out=hs_raw[32 * Q:32 * Q + 4, :, :], in_=h_scales[:, 4 * Q:4 * Q + 4, :].rearrange("g r c -> r g c"))
+        load_h(0)
+        load_h(1)
+        nc.sync.dma_start(out=t_rows[0:2, :], in_=slope.rearrange("(g c) -> g c", g=2))
+        nc.sync.dma_start(out=t_rows[2:4, :], in_=intercept.rearrange("(g c) -> g c", g=2))
+        nc.sync.dma_start(out=t_rows[4:6, :], in_=trait_scale.rearrange("(g c) -> g c", g=2))
+        nc.sync.dma_start(out=t_rows[6:7, :], in_=ancestry.rearrange("(g c) -> g c", g=1))
+        load_l(3)
+        load_c(1)
+        load_h(2)
+        load_h(3)
+
+        def sort_h(G):
+            nc.vector.tensor_copy(
+                out=h_st[G][:].bitcast(I32).rearrange("p g (t q r) -> p g t q r", t=4, q=16),
+                in_=h_raw[G][:].rearrange("p g (q t r) -> p g t q r", t=4, q=16))
+            nc.vector.tensor_copy(
+                out=hs_st[G][:].bitcast(I32).rearrange("p g (t q r) -> p g t q r", t=4, q=16),
+                in_=hs_raw[:, :, P * G:P * (G + 1)].rearrange("p g (q t r) -> p g t q r", t=4, q=16))
+
+        def sort_l(G):
+            nc.vector.tensor_copy(
+                out=l_st[G][:].rearrange("p (t q r) -> p t q r", t=4, q=16),
+                in_=l_raw[G][:].rearrange("p (q t r) -> p t q r", t=4, q=16))
+
+        def sort_l_scales():
+            nc.vector.tensor_copy(
+                out=ls_st[:].bitcast(I32).rearrange("p (t q r) -> p t q r", t=4, q=16),
+                in_=ls_raw[:].rearrange("p (q t r) -> p t q r", t=4, q=16))
+
+        x_banks = {}
+
+        def turn_x(i):
+            words = x_raw[i // 2][:, i % 2, :].bitcast(F32)
+            x_banks[i] = acc_bank("x_bank%d" % i, i, [P, 2, 2, P])
+            for g in range(2):
+                for u in range(2):
+                    nc.tensor.transpose(x_banks[i][:, g, u, :], words[:, 256 * g + u:256 * (g + 1):2], ident[:])
+
+        def gather_x(i):
+            nc.scalar.copy(out=x_t[:, :, P * i:P * (i + 1), :], in_=x_banks[i][:].rearrange("p g u r -> p g r u"))
+
+        def quantize_x(g):
+            nc.vector.quantize_mx(out=x_codes[g][:].bitcast(FP8X4), scales=x_sc[g][:],
+                                  in_=x_t[:, g, :, :].rearrange("p n u -> p (n u)").bitcast(BF16))
+
+        c_grouped = {}
+
+        def prepare_c_interleave(g, on_scalar=False):
+            c_grouped[g] = flow.tile([P, W, 4], BF16, name="c_grouped%d" % g, tag="grouped", bufs=4, align_bytes=64)
+            for h in range(2):
+                (nc.scalar.copy if on_scalar else nc.vector.tensor_copy)(
+                    out=c_grouped[g][:, 256 * h:256 * (h + 1), :].rearrange("p (j m) f -> p j m f", j=2),
+                    in_=c_raw[g][:].rearrange("p f (m j) -> p j m f", j=4)[:, 2 * h:2 * h + 2, :, :])
+
+        def prepare_c_quantize(g):
+            for h in range(2):
+                nc.vector.quantize_mx(out=c_codes[g][:, 256 * h:256 * (h + 1)].bitcast(FP8X4), scales=c_sc[g][:, 256 * h:256 * (h + 1)],
+                                      in_=c_grouped[g][:, 256 * h:256 * (h + 1), :].rearrange("p c f -> p (c f)"))
+
+        def prepare_c_half(h):
+            if h == 0:
+                c_grouped[0] = flow.tile([P, W, 4], BF16, name="c_grouped0", tag="grouped", bufs=4, align_bytes=64)
+            nc.vector.tensor_copy(out=c_grouped[0][:, 256 * h:256 * (h + 1), :].rearrange("p (j m) f -> p j m f", j=4),
+                                  in_=c_raw[0][h][:].rearrange("p f (m j) -> p j m f", j=4))
+
+        def quantize_c_half(h):
+            nc.vector.quantize_mx(out=c_codes[0][:, 256 * h:256 * (h + 1)].bitcast(FP8X4), scales=c_sc[0][:, 256 * h:256 * (h + 1)],
+                                  in_=c_grouped[0][:, 256 * h:256 * (h + 1), :].rearrange("p c f -> p (c f)"))
+
+        def variant_factors(rows, in_order, cols, name):
+            nc.scalar.activation(out=in_order[0:4, :, :].rearrange("p t (q r) -> p t q r", r=8),
+                                 in_=rows[:].rearrange("p (q t r) -> p t q r", t=4, r=8), func=ACT.Copy)
+            bank = rot_bank(name, [P, 4, P])
+            for t in range(4):
+                nc.tensor.transpose(bank[:, t, :], in_order[:, t, :], ident[:])
+            nc.scalar.copy(out=cols[:], in_=bank[:, :, 0:4].rearrange("p t i -> p i t"))
+
+        staged = {}
+
+        def label(key):
+            return "".join(str(part) for part in key)
+
+        def first_stage(key, t):
+            G = key[-1]
+            bank = rot_bank("bank_%s%d" % (label(key), t), [P, W])
+            if key[0] == "D":
+                for g in range(2):
+                    nc.tensor.matmul_mx(out=bank[:], lhsT=h_st[G][:, g, 256 * t:256 * (t + 1)].bitcast(FP4X4),
+                                        lhsT_scale=hs_st[G][:, g, P * t:P * (t + 1)],
+                                        rhs=x_codes[g][:].bitcast(FP8X4), rhs_scale=x_sc[g][:],
+                                        start=(g == 0), stop=(g == 1))
+                factor = d_cols[:, G, t:t + 1]
+            else:
+                g = key[1]
+                nc.tensor.matmul_mx(out=bank[:], lhsT=l_st[G][:, P * t:P * (t + 1)].bitcast(FP8X4),
+                                    lhsT_scale=ls_st[4 * G:, P * t:P * (t + 1)],
+                                    rhs=c_codes[g][:].bitcast(FP8X4), rhs_scale=c_sc[g][:],
+                                    start=True, stop=True)
+                factor = v_cols[:, G, t:t + 1]
+            if t == 0:
+                staged[key] = flow.tile([P, 4, W], BF16, name="staged_%s" % label(key), tag="staged", bufs=4, align_bytes=64)
+            if key[:2] == ("B", 0):
+                nc.scalar.activation(out=staged[key][:, t, :].rearrange("p (j h m) -> p h j m", j=4, h=2),
+                                     in_=bank[:].rearrange("p (h j m) -> p h j m", j=4, h=2), func=ACT.Copy, scale=factor)
+            else:
+                nc.scalar.activation(out=staged[key][:, t, :], in_=bank[:], func=ACT.Copy, scale=factor)
+
+        def first_stage_half(G, h, g=1):
+            cols = slice(256 * h, 256 * (h + 1))
+            if h == 0:
+                staged["B", g, G] = flow.tile([P, 4, W], BF16, name="staged_B%d%d" % (g, G), tag="staged", bufs=4, align_bytes=64)
+            for pair in range(2):
+                bank = rot_bank("bank_B%d%d_%d%d" % (g, G, h, pair), [P, 2, 256])
+                for u in range(2):
+                    t = 2 * pair + u
+                    nc.tensor.matmul_mx(out=bank[:, u, :], lhsT=l_st[G][:, P * t:P * (t + 1)].bitcast(FP8X4),
+                                        lhsT_scale=ls_st[4 * G:, P * t:P * (t + 1)],
+                                        rhs=c_codes[g][:, cols].bitcast(FP8X4), rhs_scale=c_sc[g][:, cols],
+                                        start=True, stop=True)
+                for u in range(2):
+                    t = 2 * pair + u
+                    if g == 0:
+                        nc.scalar.activation(out=staged["B", g, G][:, t, :].rearrange("p (j h m) -> p h j m", j=4, h=2)[:, h, :, :],
+                                             in_=bank[:, u, :].rearrange("p (j m) -> p j m", j=4), func=ACT.Copy, scale=v_cols[:, G, t:t + 1])
+                    else:
+                        nc.scalar.activation(out=staged["B", g, G][:, t, cols], in_=bank[:, u, :], func=ACT.Copy, scale=v_cols[:, G, t:t + 1])
+
+        def interleave(dst, src, h, on_scalar=False):
+            (nc.scalar.copy if on_scalar else nc.vector.tensor_copy)(
+                out=dst[:, 256 * h:256 * (h + 1), :].rearrange("p (c i) t -> p c t i", i=4),
+                in_=src[:, :, 256 * h:256 * (h + 1)].rearrange("p t (c i) -> p c t i", i=4))
+
+        def half(tiles, h):
+            return tiles[h][:] if isinstance(tiles, list) else tiles[:, 256 * h:256 * (h + 1)]
+
+        grouped = {}
+
+        def regroup(key, src, h, on_scalar=False):
+            if key not in grouped:
+                grouped[key] = flow.tile([P, W, 4], BF16, name="grouped_%s" % label(key), tag="grouped", bufs=4, align_bytes=64)
+            interleave(grouped[key], src, h, on_scalar)
+
+        def quantize(key, dst_codes, dst_scales, h):
+            nc.vector.quantize_mx(out=half(dst_codes, h).bitcast(FP8X4), scales=half(dst_scales, h),
+                                  in_=grouped[key][:, 256 * h:256 * (h + 1), :].rearrange("p c t -> p (c t)"))
+
+        def finish_group(key):
+            for h in range(2):
+                regroup(key, staged[key], h)
+            for h in range(2):
+                quantize(key, codes[key], scales[key], h)
+
+        def direct(key, c):
+            g, G = key[1], key[2]
+            cols = slice(P * c, P * (c + 1))
+            bank = rot_bank("bank_%s%d" % (label(key), c), [P, 4, P])
+            for t in range(4):
+                nc.tensor.matmul_mx(out=bank[:, t, :], lhsT=l_st[G][:, P * t:P * (t + 1)].bitcast(FP8X4),
+                                    lhsT_scale=ls_st[4 * G:, P * t:P * (t + 1)],
+                                    rhs=c_codes[g][:, cols].bitcast(FP8X4), rhs_scale=c_sc[g][:, cols],
+                                    start=True, stop=True)
+            if key not in grouped:
+                grouped[key] = flow.tile([P, W, 4], BF16, name="grouped_%s" % label(key), tag="grouped", bufs=4, align_bytes=64)
+            nc.vector.tensor_tensor(out=grouped[key][:].rearrange("p (j h m) t -> p h j m t", j=4, h=2)[:, c // 2, 2 * (c % 2):2 * (c % 2) + 2, :, :],
+                                    in0=bank[:].rearrange("p t (j m) -> p j m t", j=2),
+                                    in1=v_cols[:, G, :].unsqueeze(1).unsqueeze(1).to_broadcast([P, 2, 64, 4]), op=ALU.mult)
+
+        def quantize_group(key):
+            for h in range(2):
+                quantize(key, codes[key], scales[key], h)
+
+        acc = {}
+
+        def second_stage(g, G, j):
+            if G == 0:
+                acc[g, j] = acc_bank("acc%d_%d" % (g, j), j, [P, N])
+            cols = slice(P * (j % 2), P * (j % 2 + 1))
+            nc.tensor.matmul_mx(out=acc[g, j][:], lhsT=codes["B", g, G][j // 2][:, cols].bitcast(FP8X4),
+                                lhsT_scale=scales["B", g, G][j // 2][:, cols],
+                                rhs=codes["D", G][:].bitcast(FP8X4), rhs_scale=scales["D", G][:],
+                                start=(G == 0), stop=(G == 3))
+
+        expected = {}
+
+        def make_expected(g, j, on_scalar):
+            c = 4 * g + j
+            expected[g, j] = flow.tile([P, N], F32, name="expected%d%d" % (g, j), tag="expected", bufs=4)
+            if on_scalar:
+                nc.scalar.activation(out=expected[g, j][:], in_=anc_all[:], func=ACT.Identity,
+                                     scale=ab_col[:, 0, c:c + 1], bias=ab_col[:, 1, c:c + 1])
+            else:
+                nc.gpsimd.tensor_scalar(out=expected[g, j][:], in0=anc_all[:], scalar1=ab_col[:, 0, c:c + 1],
+                                        scalar2=ab_col[:, 1, c:c + 1], op0=ALU.mult, op1=ALU.add)
+
+        def adjust(g, j, cols):
+            nc.vector.scalar_tensor_tensor(out=y_t[g][:, j, cols], in0=acc[g, j][:, cols], scalar=t_cols[:, 4 + g, j:j + 1],
+                                           in1=expected[g, j][:, cols], op0=ALU.mult, op1=ALU.subtract)
+
+        def planes(g):
+            for h in range(2):
+                regroup(("Y", g), y_t[g], h)
+            for h in range(2):
+                quantize(("Y", g), y_codes[g], y_sc[:, g, :], h)
+            nc.sync.dma_start(out=out_1[g].rearrange("p m t -> p (m t)").bitcast(I32), in_=y_codes[g][:])
+
+        def turn_y(g, i):
+            bank = rot_bank("y_bank%d_%d" % (g, i), [P, 4, P])
+            for j in range(4):
+                nc.tensor.transpose(bank[:, j, :], y_t[g][:, j, P * i:P * (i + 1)], ident[:])
+            rows = flow.tile([P, P, 4], F32, name="y_rows%d_%d" % (g, i), tag="y_rows", bufs=8)
+            nc.scalar.copy(out=rows[:], in_=bank[:].rearrange("n j p -> n p j"))
+            nc.sync.dma_start(out=out_0[P * i:P * (i + 1), W * g:W * (g + 1)], in_=rows[:].rearrange("n p j -> n (p j)"))
+
+        everyone = slice(0, N)
+
+        def trait_vectors_turn():
+            nc.vector.tensor_copy(out=t_wide[0:7, :].rearrange("p (j m) -> p j m", j=4), in_=t_rows[:].rearrange("p (m j) -> p j m", j=4))
+            t_bank = rot_bank("t_bank", [P, 4, P])
+            for j in range(4):
+                nc.tensor.transpose(t_bank[:, j, :], t_wide[:, P * j:P * (j + 1)], ident[:])
+            return t_bank
+
+        def trait_vectors_gather(t_bank):
+            nc.vector.tensor_copy(out=t_cols[:], in_=t_bank[:, :, 0:7].rearrange("p j i -> p i j"))
+
+        def spread_ancestry():
+            anc_bank = rot_bank("anc_bank", [P, 4, P])
+            for j in range(4):
+                nc.tensor.transpose(anc_bank[:, j, :], t_cols[:, 6, j:j + 1].to_broadcast([P, P]), ident[:])
+            nc.scalar.copy(out=anc_all[:].rearrange("p (r j) -> p r j", j=4), in_=anc_bank[:].rearrange("p j r -> p r j"))
+
+        def trait_products():
+            nc.vector.tensor_tensor(out=ab_col[:], in0=t_cols[:, 0:4, :].rearrange("p (a g) j -> p a (g j)", a=2),
+                                    in1=t_cols[:, 4:6, :].rearrange("p g j -> p (g j)").unsqueeze(1).to_broadcast([P, 2, 8]), op=ALU.mult)
+
+        B = lambda g, G: ("B", g, G)
+        Dk = lambda G: ("D", G)
+        variant_factors(v_rows, v_sorted, v_cols, "v_bank")
+        prepare_c_half(0)
+        sort_l(0)
+        quantize_c_half(0)
+        sort_l_scales()
+        first_stage_half(0, 0, 0)
+        prepare_c_half(1)
+        sort_l(1)
+        quantize_c_half(1)
+        first_stage_half(0, 1, 0)
+        direct(B(0, 1), 0)
+        direct(B(0, 1), 1)
+        turn_x(0)
+        gather_x(0)
+        turn_x(1)
+        gather_x(1)
+        direct(B(0, 1), 2)
+        direct(B(0, 1), 3)
+        variant_factors(d_rows, d_sorted, d_cols, "d_bank")
+        turn_x(2)
+        turn_x(3)
+        gather_x(2)
+        gather_x(3)
+        sort_l(2)
+        quantize_group(B(0, 1))
+        sort_h(0)
+        regroup(B(0, 0), staged[B(0, 0)], 0)
+        for t in range(4):
+            first_stage(B(0, 2), t)
+        quantize_x(0)
+        quantize_x(1)
+        regroup(B(0, 0), staged[B(0, 0)], 1)
+        sort_h(1)
+        quantize_group(B(0, 0))
+        for t in range(4):
+            first_stage(Dk(0), t)
+        t_bank = trait_vectors_turn()
+        finish_group(B(0, 2))
+        trait_vectors_gather(t_bank)
+        sort_h(2)
+        sort_l(3)
+        first_stage(Dk(1), 0)
+        first_stage(Dk(1), 1)
+        spread_ancestry()
+        first_stage(Dk(1), 2)
+        first_stage(Dk(1), 3)
+        finish_group(Dk(0))
+        sort_h(3)
+        prepare_c_interleave(1, True)
+        trait_products()
+        for j in range(4):
+            make_expected(0, j, False)
+        for t in range(4):
+            direct(B(0, 3), t)
+            first_stage(Dk(2), t)
+        quantize_group(B(0, 3))
+        prepare_c_quantize(1)
+        finish_group(Dk(1))
+        for t in range(4):
+            second_stage(0, 0, t)
+            first_stage(Dk(3), t)
+        finish_group(Dk(2))
+        for t in range(4):
+            second_stage(0, 1, t)
+        for t in range(4):
+            first_stage(B(1, 0), t)
+            second_stage(0, 2, t)
+        finish_group(Dk(3))
+        for t in range(4):
+            first_stage(B(1, 1), t)
+        for t in range(4):
+            second_stage(0, 3, t)
+        finish_group(B(1, 0))
+        b1, b2, b3 = ("B", 1, 1), ("B", 1, 2), ("B", 1, 3)
+        for j in range(4):
+            adjust(0, j, everyone)
+            make_expected(1, j, j == 3)
+        first_stage_half(2, 0)
+        first_stage_half(3, 0)
+        finish_group(b1)
+        for j in range(2):
+            second_stage(1, 0, j)
+        first_stage_half(2, 1)
+        regroup(b2, staged[b2], 0)
+        regroup(b3, staged[b3], 0)
+        quantize(b2, codes[b2], scales[b2], 0)
+        quantize(b3, codes[b3], scales[b3], 0)
+        for j in range(2, 4):
+            second_stage(1, 0, j)
+        first_stage_half(3, 1)
+        for j in range(4):
+            second_stage(1, 1, j)
+        for i in range(2):
+            turn_y(0, i)
+        for j in range(2):
+            second_stage(1, 2, j)
+            second_stage(1, 3, j)
+        regroup(b2, staged[b2], 1)
+        regroup(b3, staged[b3], 1)
+        quantize(b2, codes[b2], scales[b2], 1)
+        quantize(b3, codes[b3], scales[b3], 1)
+        adjust(1, 0, everyone)
+        adjust(1, 1, everyone)
+        for i in range(2, 4):
+            turn_y(0, i)
+        regroup(("Y", 0), y_t[0], 0, True)
+        regroup(("Y", 0), y_t[0], 1, True)
+        for j in range(2, 4):
+            second_stage(1, 2, j)
+            second_stage(1, 3, j)
+        for h in range(2):
+            for j in range(2, 4):
+                adjust(1, j, slice(256 * h, 256 * (h + 1)))
+        regroup(("Y", 1), y_t[1], 0)
+        for h in range(2):
+            quantize(("Y", 0), y_codes[0], y_sc[:, 0, :], h)
+        turn_y(1, 0)
+        nc.sync.dma_start(out=out_1[0].rearrange("p m t -> p (m t)").bitcast(I32), in_=y_codes[0][:])
+        for i in range(1, 4):
+            turn_y(1, i)
+        regroup(("Y", 1), y_t[1], 1)
+        for h in range(2):
+            quantize(("Y", 1), y_codes[1], y_sc[:, 1, :], h)
+        nc.sync.dma_start(out=out_1[1].rearrange("p m t -> p (m t)").bitcast(I32), in_=y_codes[1][:])
+        for Q in range(4):
+            nc.scalar.dma_start(out=out_2[:, 4 * Q:4 * Q + 4, :].rearrange("g r n -> r g n").bitcast(I32),
+                                in_=y_sc[32 * Q:32 * Q + 4, :, :].bitcast(I32))

@@ -29,7 +29,7 @@ def tile_ancestry_adjusted_polygenic_scores_k4_kernel(
         keep = ctx.enter_context(tc.tile_pool(name="keep", bufs=1))
         flow = ctx.enter_context(tc.tile_pool(name="flow", bufs=1))
         psum = ctx.enter_context(tc.psum_pool(name="psum", bufs=1))
-        ctx.enter_context(tc.manual_schedule(engines={mybir.EngineType.SP}))
+        ctx.enter_context(tc.manual_schedule())
 
         def kept(name, shape, dtype):
             return keep.tile(shape, dtype, name=name, align_bytes=64)
@@ -55,12 +55,9 @@ def tile_ancestry_adjusted_polygenic_scores_k4_kernel(
         v_rows = kept("v_rows", [4, W], BF16)
         v_sorted = kept("v_sorted", [P, 4, P], F32)
         v_cols = kept("v_cols", [P, 4, 4], F32)
-        d_rows = kept("d_rows", [4, W], BF16)
+        d_rows = kept("d_rows", [39, W], BF16)
         d_sorted = kept("d_sorted", [P, 4, P], F32)
-        d_cols = kept("d_cols", [P, 4, 4], F32)
-        t_rows = kept("t_rows", [7, W], BF16)
-        t_wide = kept("t_wide", [P, W], F32)
-        t_cols = kept("t_cols", [P, 7, 4], F32)
+        d_cols = kept("d_cols", [P, 2, 7, 4], F32)
         anc_all = kept("anc_all", [P, N], F32)
         ab_col = kept("ab_col", [P, 2, 8], F32)
         h_st = [kept("h_st%d" % G, [P, 2, 1024], U8) for G in range(4)]
@@ -87,8 +84,7 @@ def tile_ancestry_adjusted_polygenic_scores_k4_kernel(
         nc.vector.memset(v_sorted[:], 0.0)
         nc.vector.memset(ls_raw[:], 0)
         nc.vector.memset(hs_raw[:], 0)
-        nc.vector.memset(d_sorted[:], 0.0)
-        nc.scalar.activation(out=t_wide[:], in_=v_sorted[:].rearrange("p t m -> p (t m)"), func=ACT.Copy)
+        nc.scalar.activation(out=d_sorted[:], in_=v_sorted[:], func=ACT.Copy)
 
         def load_x(i):
             nc.sync.dma_start(out=x_raw[i][:], in_=x[256 * i:256 * (i + 1), :].rearrange("(i p) k -> p i k", p=P))
@@ -105,27 +101,39 @@ def tile_ancestry_adjusted_polygenic_scores_k4_kernel(
         def load_c_half(h):
             nc.sync.dma_start(out=c_raw[0][h][:], in_=trait_factors[:, 256 * h:256 * (h + 1)].rearrange("(p f) c -> p f c", f=4))
 
+        def load_rows(first, rows, vector):
+            nc.sync.dma_start(out=d_rows[first:first + rows, :], in_=vector.rearrange("(g c) -> g c", g=rows))
+
+        def load_l_scales():
+            for Q in range(4):
+                nc.sync.dma_start(out=ls_raw[32 * Q:32 * Q + 16, :], in_=l_scales[4 * Q:4 * Q + 4, :].rearrange("r (G c) -> G r c", G=4))
+
+        def load_h_scales():
+            for Q in range(4):
+                nc.sync.dma_start(out=hs_raw[32 * Q:32 * Q + 4, :, :], in_=h_scales[:, 4 * Q:4 * Q + 4, :].rearrange("g r c -> r g c"))
+
+        def load_small():
+            load_rows(0, 4, dosage_scale)
+            load_rows(32, 2, slope)
+            load_rows(34, 2, intercept)
+            load_rows(36, 2, trait_scale)
+            load_rows(38, 1, ancestry)
+
         nc.sync.dma_start(out=v_rows[:], in_=variant_weight.rearrange("(G c) -> G c", G=4))
         load_c_half(0)
         load_l(0)
-        for Q in range(4):
-            nc.sync.dma_start(out=ls_raw[32 * Q:32 * Q + 16, :], in_=l_scales[4 * Q:4 * Q + 4, :].rearrange("r (G c) -> G r c", G=4))
+        load_l_scales()
         load_c_half(1)
         load_l(1)
-        nc.sync.dma_start(out=d_rows[:], in_=dosage_scale.rearrange("(G c) -> G c", G=4))
         load_x(0)
         load_x(1)
+        load_h_scales()
         load_l(2)
-        for Q in range(4):
-            nc.sync.dma_start(out=hs_raw[32 * Q:32 * Q + 4, :, :], in_=h_scales[:, 4 * Q:4 * Q + 4, :].rearrange("g r c -> r g c"))
         load_h(0)
+        load_small()
         load_h(1)
-        nc.sync.dma_start(out=t_rows[0:2, :], in_=slope.rearrange("(g c) -> g c", g=2))
-        nc.sync.dma_start(out=t_rows[2:4, :], in_=intercept.rearrange("(g c) -> g c", g=2))
-        nc.sync.dma_start(out=t_rows[4:6, :], in_=trait_scale.rearrange("(g c) -> g c", g=2))
-        nc.sync.dma_start(out=t_rows[6:7, :], in_=ancestry.rearrange("(g c) -> g c", g=1))
-        load_l(3)
         load_c(1)
+        load_l(3)
         load_h(2)
         load_h(3)
 
@@ -165,9 +173,10 @@ def tile_ancestry_adjusted_polygenic_scores_k4_kernel(
 
         c_grouped = {}
 
-        def prepare_c_interleave(g, on_scalar=False):
-            c_grouped[g] = flow.tile([P, W, 4], BF16, name="c_grouped%d" % g, tag="grouped", bufs=4, align_bytes=64)
-            for h in range(2):
+        def prepare_c_interleave(g, on_scalar, h):
+            if h == 0:
+                c_grouped[g] = flow.tile([P, W, 4], BF16, name="c_grouped%d" % g, tag="grouped", bufs=4, align_bytes=64)
+            if True:
                 (nc.scalar.copy if on_scalar else nc.vector.tensor_copy)(
                     out=c_grouped[g][:, 256 * h:256 * (h + 1), :].rearrange("p (j m) f -> p j m f", j=2),
                     in_=c_raw[g][:].rearrange("p f (m j) -> p j m f", j=4)[:, 2 * h:2 * h + 2, :, :])
@@ -187,13 +196,18 @@ def tile_ancestry_adjusted_polygenic_scores_k4_kernel(
             nc.vector.quantize_mx(out=c_codes[0][:, 256 * h:256 * (h + 1)].bitcast(FP8X4), scales=c_sc[0][:, 256 * h:256 * (h + 1)],
                                   in_=c_grouped[0][:, 256 * h:256 * (h + 1), :].rearrange("p c f -> p (c f)"))
 
-        def variant_factors(rows, in_order, cols, name):
-            nc.scalar.activation(out=in_order[0:4, :, :].rearrange("p t (q r) -> p t q r", r=8),
-                                 in_=rows[:].rearrange("p (q t r) -> p t q r", t=4, r=8), func=ACT.Copy)
+        def sort_variant_rows(rows, in_order):
+            nc.vector.tensor_copy(out=in_order[0:4, :, :].rearrange("p t (q r) -> p t q r", r=8),
+                                  in_=rows[0:4, :].rearrange("p (q t r) -> p t q r", t=4, r=8))
+
+        def sort_trait_rows():
+            nc.vector.tensor_copy(out=d_sorted[32:39, :, :], in_=d_rows[32:39, :].rearrange("p (m j) -> p j m", j=4))
+
+        def turn_rows(in_order, name):
             bank = rot_bank(name, [P, 4, P])
             for t in range(4):
                 nc.tensor.transpose(bank[:, t, :], in_order[:, t, :], ident[:])
-            nc.scalar.copy(out=cols[:], in_=bank[:, :, 0:4].rearrange("p t i -> p i t"))
+            return bank
 
         staged = {}
 
@@ -209,7 +223,7 @@ def tile_ancestry_adjusted_polygenic_scores_k4_kernel(
                                         lhsT_scale=hs_st[G][:, g, P * t:P * (t + 1)],
                                         rhs=x_codes[g][:].bitcast(FP8X4), rhs_scale=x_sc[g][:],
                                         start=(g == 0), stop=(g == 1))
-                factor = d_cols[:, G, t:t + 1]
+                factor = d_cols[:, 0, G, t:t + 1]
             else:
                 g = key[1]
                 nc.tensor.matmul_mx(out=bank[:], lhsT=l_st[G][:, P * t:P * (t + 1)].bitcast(FP8X4),
@@ -273,7 +287,10 @@ def tile_ancestry_adjusted_polygenic_scores_k4_kernel(
         def direct(key, c):
             g, G = key[1], key[2]
             cols = slice(P * c, P * (c + 1))
-            bank = rot_bank("bank_%s%d" % (label(key), c), [P, 4, P])
+            if G == 3:
+                bank = acc_bank("bank_%s%d" % (label(key), c), c, [P, 4, P])
+            else:
+                bank = rot_bank("bank_%s%d" % (label(key), c), [P, 4, P])
             for t in range(4):
                 nc.tensor.matmul_mx(out=bank[:, t, :], lhsT=l_st[G][:, P * t:P * (t + 1)].bitcast(FP8X4),
                                     lhsT_scale=ls_st[4 * G:, P * t:P * (t + 1)],
@@ -304,7 +321,10 @@ def tile_ancestry_adjusted_polygenic_scores_k4_kernel(
 
         def make_expected(g, j, on_scalar):
             c = 4 * g + j
-            expected[g, j] = flow.tile([P, N], F32, name="expected%d%d" % (g, j), tag="expected", bufs=4)
+            if on_scalar:
+                expected[g, j] = kept("expected%d%d" % (g, j), [P, N], F32)
+            else:
+                expected[g, j] = flow.tile([P, N], F32, name="expected%d%d" % (g, j), tag="expected", bufs=4)
             if on_scalar:
                 nc.scalar.activation(out=expected[g, j][:], in_=anc_all[:], func=ACT.Identity,
                                      scale=ab_col[:, 0, c:c + 1], bias=ab_col[:, 1, c:c + 1])
@@ -313,7 +333,7 @@ def tile_ancestry_adjusted_polygenic_scores_k4_kernel(
                                         scalar2=ab_col[:, 1, c:c + 1], op0=ALU.mult, op1=ALU.add)
 
         def adjust(g, j, cols):
-            nc.vector.scalar_tensor_tensor(out=y_t[g][:, j, cols], in0=acc[g, j][:, cols], scalar=t_cols[:, 4 + g, j:j + 1],
+            nc.vector.scalar_tensor_tensor(out=y_t[g][:, j, cols], in0=acc[g, j][:, cols], scalar=d_cols[:, 1, 4 + g, j:j + 1],
                                            in1=expected[g, j][:, cols], op0=ALU.mult, op1=ALU.subtract)
 
         def planes(g):
@@ -333,29 +353,21 @@ def tile_ancestry_adjusted_polygenic_scores_k4_kernel(
 
         everyone = slice(0, N)
 
-        def trait_vectors_turn():
-            nc.vector.tensor_copy(out=t_wide[0:7, :].rearrange("p (j m) -> p j m", j=4), in_=t_rows[:].rearrange("p (m j) -> p j m", j=4))
-            t_bank = rot_bank("t_bank", [P, 4, P])
-            for j in range(4):
-                nc.tensor.transpose(t_bank[:, j, :], t_wide[:, P * j:P * (j + 1)], ident[:])
-            return t_bank
-
-        def trait_vectors_gather(t_bank):
-            nc.vector.tensor_copy(out=t_cols[:], in_=t_bank[:, :, 0:7].rearrange("p j i -> p i j"))
-
         def spread_ancestry():
             anc_bank = rot_bank("anc_bank", [P, 4, P])
             for j in range(4):
-                nc.tensor.transpose(anc_bank[:, j, :], t_cols[:, 6, j:j + 1].to_broadcast([P, P]), ident[:])
+                nc.tensor.transpose(anc_bank[:, j, :], d_cols[:, 1, 6, j:j + 1].to_broadcast([P, P]), ident[:])
             nc.scalar.copy(out=anc_all[:].rearrange("p (r j) -> p r j", j=4), in_=anc_bank[:].rearrange("p j r -> p r j"))
 
         def trait_products():
-            nc.vector.tensor_tensor(out=ab_col[:], in0=t_cols[:, 0:4, :].rearrange("p (a g) j -> p a (g j)", a=2),
-                                    in1=t_cols[:, 4:6, :].rearrange("p g j -> p (g j)").unsqueeze(1).to_broadcast([P, 2, 8]), op=ALU.mult)
+            nc.vector.tensor_tensor(out=ab_col[:], in0=d_cols[:, 1, 0:4, :].rearrange("p (a g) j -> p a (g j)", a=2),
+                                    in1=d_cols[:, 1, 4:6, :].rearrange("p g j -> p (g j)").unsqueeze(1).to_broadcast([P, 2, 8]), op=ALU.mult)
 
         B = lambda g, G: ("B", g, G)
         Dk = lambda G: ("D", G)
-        variant_factors(v_rows, v_sorted, v_cols, "v_bank")
+        sort_variant_rows(v_rows, v_sorted)
+        v_bank = turn_rows(v_sorted, "v_bank")
+        nc.scalar.copy(out=v_cols[:], in_=v_bank[:, :, 0:4].rearrange("p t i -> p i t"))
         prepare_c_half(0)
         sort_l(0)
         quantize_c_half(0)
@@ -367,63 +379,66 @@ def tile_ancestry_adjusted_polygenic_scores_k4_kernel(
         first_stage_half(0, 1, 0)
         direct(B(0, 1), 0)
         direct(B(0, 1), 1)
-        turn_x(0)
-        gather_x(0)
-        turn_x(1)
-        gather_x(1)
+        for i in range(2):
+            turn_x(i)
+            gather_x(i)
+        regroup(B(0, 0), staged[B(0, 0)], 0)
         direct(B(0, 1), 2)
         direct(B(0, 1), 3)
-        variant_factors(d_rows, d_sorted, d_cols, "d_bank")
-        turn_x(2)
-        turn_x(3)
-        gather_x(2)
-        gather_x(3)
+        for i in range(2, 4):
+            turn_x(i)
+            gather_x(i)
         sort_l(2)
-        quantize_group(B(0, 1))
         sort_h(0)
-        regroup(B(0, 0), staged[B(0, 0)], 0)
         for t in range(4):
             first_stage(B(0, 2), t)
         quantize_x(0)
+        sort_variant_rows(d_rows, d_sorted)
+        sort_trait_rows()
         quantize_x(1)
-        regroup(B(0, 0), staged[B(0, 0)], 1)
+        d_bank = turn_rows(d_sorted, "d_bank")
+        nc.scalar.copy(out=d_cols[:], in_=d_bank[:, :, 0:64].rearrange("p t (a i) -> p a i t", a=2)[:, :, 0:7, :])
         sort_h(1)
+        quantize_group(B(0, 1))
+        regroup(B(0, 0), staged[B(0, 0)], 1)
+        sort_l(3)
         quantize_group(B(0, 0))
         for t in range(4):
             first_stage(Dk(0), t)
-        t_bank = trait_vectors_turn()
-        finish_group(B(0, 2))
-        trait_vectors_gather(t_bank)
-        sort_h(2)
-        sort_l(3)
-        first_stage(Dk(1), 0)
-        first_stage(Dk(1), 1)
         spread_ancestry()
-        first_stage(Dk(1), 2)
-        first_stage(Dk(1), 3)
+        finish_group(B(0, 2))
+        sort_h(2)
+        for t in range(2):
+            first_stage(Dk(1), t)
         finish_group(Dk(0))
-        sort_h(3)
-        prepare_c_interleave(1, True)
         trait_products()
         for j in range(4):
             make_expected(0, j, False)
+        prepare_c_interleave(1, True, 0)
+        first_stage(Dk(1), 2)
+        first_stage(Dk(1), 3)
+        prepare_c_interleave(1, True, 1)
         for t in range(4):
             direct(B(0, 3), t)
+        for t in range(4):
             first_stage(Dk(2), t)
+        sort_h(3)
         quantize_group(B(0, 3))
+        make_expected(1, 3, True)
+        regroup(Dk(1), staged[Dk(1)], 0)
+        regroup(Dk(1), staged[Dk(1)], 1)
         prepare_c_quantize(1)
-        finish_group(Dk(1))
+        quantize_group(Dk(1))
         for t in range(4):
             second_stage(0, 0, t)
             first_stage(Dk(3), t)
         finish_group(Dk(2))
         for t in range(4):
-            second_stage(0, 1, t)
-        for t in range(4):
             first_stage(B(1, 0), t)
-            second_stage(0, 2, t)
+            second_stage(0, 1, t)
         finish_group(Dk(3))
         for t in range(4):
+            second_stage(0, 2, t)
             first_stage(B(1, 1), t)
         for t in range(4):
             second_stage(0, 3, t)
@@ -431,24 +446,27 @@ def tile_ancestry_adjusted_polygenic_scores_k4_kernel(
         b1, b2, b3 = ("B", 1, 1), ("B", 1, 2), ("B", 1, 3)
         for j in range(4):
             adjust(0, j, everyone)
-            make_expected(1, j, j == 3)
+            if j < 3:
+                make_expected(1, j, False)
         first_stage_half(2, 0)
         first_stage_half(3, 0)
         finish_group(b1)
-        for j in range(2):
-            second_stage(1, 0, j)
+        second_stage(1, 0, 0)
         first_stage_half(2, 1)
+        second_stage(1, 0, 1)
         regroup(b2, staged[b2], 0)
         regroup(b3, staged[b3], 0)
         quantize(b2, codes[b2], scales[b2], 0)
         quantize(b3, codes[b3], scales[b3], 0)
-        for j in range(2, 4):
-            second_stage(1, 0, j)
+        second_stage(1, 0, 2)
         first_stage_half(3, 1)
-        for j in range(4):
-            second_stage(1, 1, j)
+        second_stage(1, 0, 3)
+        regroup(("Y", 0), y_t[0], 0, True)
         for i in range(2):
             turn_y(0, i)
+        for j in range(4):
+            second_stage(1, 1, j)
+        regroup(("Y", 0), y_t[0], 1, True)
         for j in range(2):
             second_stage(1, 2, j)
             second_stage(1, 3, j)
@@ -460,20 +478,17 @@ def tile_ancestry_adjusted_polygenic_scores_k4_kernel(
         adjust(1, 1, everyone)
         for i in range(2, 4):
             turn_y(0, i)
-        regroup(("Y", 0), y_t[0], 0, True)
-        regroup(("Y", 0), y_t[0], 1, True)
         for j in range(2, 4):
             second_stage(1, 2, j)
             second_stage(1, 3, j)
         for h in range(2):
+            quantize(("Y", 0), y_codes[0], y_sc[:, 0, :], h)
+        nc.sync.dma_start(out=out_1[0].rearrange("p m t -> p (m t)").bitcast(I32), in_=y_codes[0][:])
+        for h in range(2):
             for j in range(2, 4):
                 adjust(1, j, slice(256 * h, 256 * (h + 1)))
         regroup(("Y", 1), y_t[1], 0)
-        for h in range(2):
-            quantize(("Y", 0), y_codes[0], y_sc[:, 0, :], h)
-        turn_y(1, 0)
-        nc.sync.dma_start(out=out_1[0].rearrange("p m t -> p (m t)").bitcast(I32), in_=y_codes[0][:])
-        for i in range(1, 4):
+        for i in range(4):
             turn_y(1, i)
         regroup(("Y", 1), y_t[1], 1)
         for h in range(2):

@@ -17,6 +17,7 @@ ACT = mybir.ActivationFunctionType
 
 P = 128
 W = 512
+SHARED = {("D", 1): "handed_d", ("D", 2): "handed_d"}
 
 
 def tile_ancestry_adjusted_polygenic_scores_k4_kernel(
@@ -55,9 +56,14 @@ def tile_ancestry_adjusted_polygenic_scores_k4_kernel(
         v_rows = kept("v_rows", [4, W], BF16)
         v_sorted = kept("v_sorted", [P, 4, P], F32)
         v_cols = kept("v_cols", [P, 4, 4], F32)
-        d_rows = kept("d_rows", [39, W], BF16)
+        d_rows = kept("d_rows", [4, W], BF16)
         d_sorted = kept("d_sorted", [P, 4, P], F32)
-        d_cols = kept("d_cols", [P, 2, 7, 4], F32)
+        d_cols = kept("d_cols", [P, 4, 4], F32)
+        slope_col = kept("slope_col", [P, 2, 4], BF16)
+        icpt_col = kept("icpt_col", [P, 2, 4], BF16)
+        ts_col = kept("ts_col", [P, 2, 4], BF16)
+        anc_raw = kept("anc_raw", [P, 4], BF16)
+        anc_col = kept("anc_col", [P, 4], F32)
         anc_all = kept("anc_all", [P, N], F32)
         ab_col = kept("ab_col", [P, 2, 8], F32)
         h_st = [kept("h_st%d" % G, [P, 2, 1024], U8) for G in range(4)]
@@ -112,12 +118,10 @@ def tile_ancestry_adjusted_polygenic_scores_k4_kernel(
             for Q in range(4):
                 nc.sync.dma_start(out=hs_raw[32 * Q:32 * Q + 4, :, :], in_=h_scales[:, 4 * Q:4 * Q + 4, :].rearrange("g r c -> r g c"))
 
-        def load_small():
-            load_rows(0, 4, dosage_scale)
-            load_rows(32, 2, slope)
-            load_rows(34, 2, intercept)
-            load_rows(36, 2, trait_scale)
-            load_rows(38, 1, ancestry)
+        def load_trait_columns():
+            nc.sync.dma_start(out=anc_raw[:], in_=ancestry.rearrange("(p j) -> p j", j=4))
+            for tile_, vector in ((ts_col, trait_scale), (slope_col, slope), (icpt_col, intercept)):
+                nc.sync.dma_start(out=tile_[:], in_=vector.rearrange("(g p j) -> p g j", g=2, j=4))
 
         nc.sync.dma_start(out=v_rows[:], in_=variant_weight.rearrange("(G c) -> G c", G=4))
         load_c_half(0)
@@ -130,11 +134,12 @@ def tile_ancestry_adjusted_polygenic_scores_k4_kernel(
         load_h_scales()
         load_l(2)
         load_h(0)
-        load_small()
+        load_rows(0, 4, dosage_scale)
         load_h(1)
-        load_c(1)
         load_l(3)
+        load_c(1)
         load_h(2)
+        load_trait_columns()
         load_h(3)
 
         def sort_h(G):
@@ -200,9 +205,6 @@ def tile_ancestry_adjusted_polygenic_scores_k4_kernel(
             nc.vector.tensor_copy(out=in_order[0:4, :, :].rearrange("p t (q r) -> p t q r", r=8),
                                   in_=rows[0:4, :].rearrange("p (q t r) -> p t q r", t=4, r=8))
 
-        def sort_trait_rows():
-            nc.vector.tensor_copy(out=d_sorted[32:39, :, :], in_=d_rows[32:39, :].rearrange("p (m j) -> p j m", j=4))
-
         def turn_rows(in_order, name):
             bank = rot_bank(name, [P, 4, P])
             for t in range(4):
@@ -223,7 +225,7 @@ def tile_ancestry_adjusted_polygenic_scores_k4_kernel(
                                         lhsT_scale=hs_st[G][:, g, P * t:P * (t + 1)],
                                         rhs=x_codes[g][:].bitcast(FP8X4), rhs_scale=x_sc[g][:],
                                         start=(g == 0), stop=(g == 1))
-                factor = d_cols[:, 0, G, t:t + 1]
+                factor = d_cols[:, G, t:t + 1]
             else:
                 g = key[1]
                 nc.tensor.matmul_mx(out=bank[:], lhsT=l_st[G][:, P * t:P * (t + 1)].bitcast(FP8X4),
@@ -271,8 +273,16 @@ def tile_ancestry_adjusted_polygenic_scores_k4_kernel(
 
         def regroup(key, src, h, on_scalar=False):
             if key not in grouped:
-                grouped[key] = flow.tile([P, W, 4], BF16, name="grouped_%s" % label(key), tag="grouped", bufs=4, align_bytes=64)
-            interleave(grouped[key], src, h, on_scalar)
+                if key in SHARED:
+                    grouped[key] = flow.tile([P, W, 4], BF16, name="grouped_%s" % label(key), tag=SHARED[key], bufs=1, align_bytes=64)
+                else:
+                    grouped[key] = flow.tile([P, W, 4], BF16, name="grouped_%s" % label(key), tag="grouped", bufs=4, align_bytes=64)
+            if on_scalar == "G":
+                cols = slice(256 * h, 256 * (h + 1))
+                nc.gpsimd.tensor_scalar(out=grouped[key][:, cols, :], in0=src[:, :, cols].rearrange("p t c -> p c t"),
+                                        scalar1=1.0, scalar2=0.0, op0=ALU.mult, op1=ALU.add)
+            else:
+                interleave(grouped[key], src, h, on_scalar)
 
         def quantize(key, dst_codes, dst_scales, h):
             nc.vector.quantize_mx(out=half(dst_codes, h).bitcast(FP8X4), scales=half(dst_scales, h),
@@ -284,11 +294,11 @@ def tile_ancestry_adjusted_polygenic_scores_k4_kernel(
             for h in range(2):
                 quantize(key, codes[key], scales[key], h)
 
-        def direct(key, c):
+        def direct(key, c, acc_slot=None):
             g, G = key[1], key[2]
             cols = slice(P * c, P * (c + 1))
-            if G == 3:
-                bank = acc_bank("bank_%s%d" % (label(key), c), c, [P, 4, P])
+            if acc_slot is not None:
+                bank = acc_bank("bank_%s%d" % (label(key), c), acc_slot, [P, 4, P])
             else:
                 bank = rot_bank("bank_%s%d" % (label(key), c), [P, 4, P])
             for t in range(4):
@@ -298,6 +308,10 @@ def tile_ancestry_adjusted_polygenic_scores_k4_kernel(
                                     start=True, stop=True)
             if key not in grouped:
                 grouped[key] = flow.tile([P, W, 4], BF16, name="grouped_%s" % label(key), tag="grouped", bufs=4, align_bytes=64)
+            if g == 1:
+                nc.vector.tensor_tensor(out=grouped[key][:, cols, :], in0=bank[:].rearrange("p t n -> p n t"),
+                                        in1=v_cols[:, G, :].unsqueeze(1).to_broadcast([P, P, 4]), op=ALU.mult)
+                return
             nc.vector.tensor_tensor(out=grouped[key][:].rearrange("p (j h m) t -> p h j m t", j=4, h=2)[:, c // 2, 2 * (c % 2):2 * (c % 2) + 2, :, :],
                                     in0=bank[:].rearrange("p t (j m) -> p j m t", j=2),
                                     in1=v_cols[:, G, :].unsqueeze(1).unsqueeze(1).to_broadcast([P, 2, 64, 4]), op=ALU.mult)
@@ -324,7 +338,7 @@ def tile_ancestry_adjusted_polygenic_scores_k4_kernel(
             if on_scalar:
                 expected[g, j] = kept("expected%d%d" % (g, j), [P, N], F32)
             else:
-                expected[g, j] = flow.tile([P, N], F32, name="expected%d%d" % (g, j), tag="expected", bufs=4)
+                expected[g, j] = flow.tile([P, N], F32, name="expected%d%d" % (g, j), tag="expected", bufs=3)
             if on_scalar:
                 nc.scalar.activation(out=expected[g, j][:], in_=anc_all[:], func=ACT.Identity,
                                      scale=ab_col[:, 0, c:c + 1], bias=ab_col[:, 1, c:c + 1])
@@ -333,12 +347,17 @@ def tile_ancestry_adjusted_polygenic_scores_k4_kernel(
                                         scalar2=ab_col[:, 1, c:c + 1], op0=ALU.mult, op1=ALU.add)
 
         def adjust(g, j, cols):
-            nc.vector.scalar_tensor_tensor(out=y_t[g][:, j, cols], in0=acc[g, j][:, cols], scalar=d_cols[:, 1, 4 + g, j:j + 1],
+            nc.vector.scalar_tensor_tensor(out=y_t[g][:, j, cols], in0=acc[g, j][:, cols], scalar=ts_col[:, g, j:j + 1],
                                            in1=expected[g, j][:, cols], op0=ALU.mult, op1=ALU.subtract)
 
         def planes(g):
             for h in range(2):
                 regroup(("Y", g), y_t[g], h)
+            for h in range(2):
+                quantize(("Y", g), y_codes[g], y_sc[:, g, :], h)
+            nc.sync.dma_start(out=out_1[g].rearrange("p m t -> p (m t)").bitcast(I32), in_=y_codes[g][:])
+
+        def store_planes(g):
             for h in range(2):
                 quantize(("Y", g), y_codes[g], y_sc[:, g, :], h)
             nc.sync.dma_start(out=out_1[g].rearrange("p m t -> p (m t)").bitcast(I32), in_=y_codes[g][:])
@@ -356,12 +375,13 @@ def tile_ancestry_adjusted_polygenic_scores_k4_kernel(
         def spread_ancestry():
             anc_bank = rot_bank("anc_bank", [P, 4, P])
             for j in range(4):
-                nc.tensor.transpose(anc_bank[:, j, :], d_cols[:, 1, 6, j:j + 1].to_broadcast([P, P]), ident[:])
+                nc.tensor.transpose(anc_bank[:, j, :], anc_col[:, j:j + 1].to_broadcast([P, P]), ident[:])
             nc.scalar.copy(out=anc_all[:].rearrange("p (r j) -> p r j", j=4), in_=anc_bank[:].rearrange("p j r -> p r j"))
 
         def trait_products():
-            nc.vector.tensor_tensor(out=ab_col[:], in0=d_cols[:, 1, 0:4, :].rearrange("p (a g) j -> p a (g j)", a=2),
-                                    in1=d_cols[:, 1, 4:6, :].rearrange("p g j -> p (g j)").unsqueeze(1).to_broadcast([P, 2, 8]), op=ALU.mult)
+            for a, vector in enumerate((slope_col, icpt_col)):
+                nc.vector.tensor_tensor(out=ab_col[:, a, :], in0=vector[:].rearrange("p g j -> p (g j)"),
+                                        in1=ts_col[:].rearrange("p g j -> p (g j)"), op=ALU.mult)
 
         B = lambda g, G: ("B", g, G)
         Dk = lambda G: ("D", G)
@@ -376,97 +396,112 @@ def tile_ancestry_adjusted_polygenic_scores_k4_kernel(
         prepare_c_half(1)
         sort_l(1)
         quantize_c_half(1)
+        direct(B(0, 1), 0, 2)
+        direct(B(0, 1), 1, 3)
         first_stage_half(0, 1, 0)
-        direct(B(0, 1), 0)
-        direct(B(0, 1), 1)
-        for i in range(2):
+        direct(B(0, 1), 2)
+        direct(B(0, 1), 3)
+        for i in range(4):
             turn_x(i)
             gather_x(i)
         regroup(B(0, 0), staged[B(0, 0)], 0)
-        direct(B(0, 1), 2)
-        direct(B(0, 1), 3)
-        for i in range(2, 4):
-            turn_x(i)
-            gather_x(i)
         sort_l(2)
+        regroup(B(0, 0), staged[B(0, 0)], 1)
         sort_h(0)
+        sort_variant_rows(d_rows, d_sorted)
         for t in range(4):
             first_stage(B(0, 2), t)
-        quantize_x(0)
-        sort_variant_rows(d_rows, d_sorted)
-        sort_trait_rows()
-        quantize_x(1)
         d_bank = turn_rows(d_sorted, "d_bank")
-        nc.scalar.copy(out=d_cols[:], in_=d_bank[:, :, 0:64].rearrange("p t (a i) -> p a i t", a=2)[:, :, 0:7, :])
+        nc.scalar.copy(out=d_cols[:], in_=d_bank[:, :, 0:4].rearrange("p t i -> p i t"))
+        quantize_x(0)
+        quantize_x(1)
         sort_h(1)
         quantize_group(B(0, 1))
-        regroup(B(0, 0), staged[B(0, 0)], 1)
         sort_l(3)
         quantize_group(B(0, 0))
         for t in range(4):
             first_stage(Dk(0), t)
-        spread_ancestry()
+        nc.vector.tensor_copy(out=anc_col[:], in_=anc_raw[:])
         finish_group(B(0, 2))
         sort_h(2)
         for t in range(2):
             first_stage(Dk(1), t)
+        spread_ancestry()
         finish_group(Dk(0))
         trait_products()
-        for j in range(4):
+        for j in range(3):
             make_expected(0, j, False)
         prepare_c_interleave(1, True, 0)
         first_stage(Dk(1), 2)
         first_stage(Dk(1), 3)
         prepare_c_interleave(1, True, 1)
         for t in range(4):
-            direct(B(0, 3), t)
+            direct(B(0, 3), t, t)
         for t in range(4):
             first_stage(Dk(2), t)
         sort_h(3)
         quantize_group(B(0, 3))
-        make_expected(1, 3, True)
         regroup(Dk(1), staged[Dk(1)], 0)
-        regroup(Dk(1), staged[Dk(1)], 1)
         prepare_c_quantize(1)
+        regroup(Dk(1), staged[Dk(1)], 1)
+        second_stage(0, 0, 0)
+        first_stage(Dk(3), 0)
+        second_stage(0, 0, 1)
+        first_stage(Dk(3), 1)
+        make_expected(0, 3, True)
         quantize_group(Dk(1))
+        regroup(Dk(2), staged[Dk(2)], 0, "G")
+        regroup(Dk(2), staged[Dk(2)], 1, "G")
+        direct(B(1, 0), 0)
+        direct(B(1, 0), 1)
+        first_stage(Dk(3), 2)
+        direct(B(1, 0), 2)
+        first_stage(Dk(3), 3)
+        direct(B(1, 0), 3)
+        regroup(Dk(3), staged[Dk(3)], 0, True)
+        second_stage(0, 0, 2)
+        second_stage(0, 0, 3)
+        quantize_group(Dk(2))
         for t in range(4):
-            second_stage(0, 0, t)
-            first_stage(Dk(3), t)
-        finish_group(Dk(2))
-        for t in range(4):
-            first_stage(B(1, 0), t)
+            first_stage(B(1, 1), t)
             second_stage(0, 1, t)
-        finish_group(Dk(3))
+        regroup(Dk(3), staged[Dk(3)], 1)
+        quantize_group(Dk(3))
+        quantize_group(B(1, 0))
         for t in range(4):
             second_stage(0, 2, t)
-            first_stage(B(1, 1), t)
+        regroup(B(1, 1), staged[B(1, 1)], 0)
         for t in range(4):
             second_stage(0, 3, t)
-        finish_group(B(1, 0))
-        b1, b2, b3 = ("B", 1, 1), ("B", 1, 2), ("B", 1, 3)
+        make_expected(1, 3, True)
+        first_stage_half(2, 0)
+        first_stage_half(3, 0)
+        b2, b3 = ("B", 1, 2), ("B", 1, 3)
         for j in range(4):
             adjust(0, j, everyone)
             if j < 3:
                 make_expected(1, j, False)
-        first_stage_half(2, 0)
-        first_stage_half(3, 0)
-        finish_group(b1)
+        regroup(B(1, 1), staged[B(1, 1)], 1)
         second_stage(1, 0, 0)
-        first_stage_half(2, 1)
         second_stage(1, 0, 1)
+        first_stage_half(2, 1)
+        second_stage(1, 0, 2)
+        second_stage(1, 0, 3)
+        for i in range(0):
+            turn_y(0, i)
+        first_stage_half(3, 1)
         regroup(b2, staged[b2], 0)
+        quantize_group(B(1, 1))
         regroup(b3, staged[b3], 0)
         quantize(b2, codes[b2], scales[b2], 0)
         quantize(b3, codes[b3], scales[b3], 0)
-        second_stage(1, 0, 2)
-        first_stage_half(3, 1)
-        second_stage(1, 0, 3)
-        regroup(("Y", 0), y_t[0], 0, True)
-        for i in range(2):
+        for i in range(0, 2):
             turn_y(0, i)
+        regroup(("Y", 0), y_t[0], 0, True)
         for j in range(4):
             second_stage(1, 1, j)
-        regroup(("Y", 0), y_t[0], 1, True)
+        for i in range(2, 4):
+            turn_y(0, i)
         for j in range(2):
             second_stage(1, 2, j)
             second_stage(1, 3, j)
@@ -474,26 +509,27 @@ def tile_ancestry_adjusted_polygenic_scores_k4_kernel(
         regroup(b3, staged[b3], 1)
         quantize(b2, codes[b2], scales[b2], 1)
         quantize(b3, codes[b3], scales[b3], 1)
+
+        regroup(("Y", 0), y_t[0], 1, True)
         adjust(1, 0, everyone)
         adjust(1, 1, everyone)
-        for i in range(2, 4):
+        for i in range(4, 4):
             turn_y(0, i)
         for j in range(2, 4):
             second_stage(1, 2, j)
             second_stage(1, 3, j)
-        for h in range(2):
-            quantize(("Y", 0), y_codes[0], y_sc[:, 0, :], h)
-        nc.sync.dma_start(out=out_1[0].rearrange("p m t -> p (m t)").bitcast(I32), in_=y_codes[0][:])
-        for h in range(2):
-            for j in range(2, 4):
-                adjust(1, j, slice(256 * h, 256 * (h + 1)))
+
+        for j in range(2, 4):
+            adjust(1, j, slice(0, 256))
+        store_planes(0)
+        for j in range(2, 4):
+            adjust(1, j, slice(256, 512))
+
         regroup(("Y", 1), y_t[1], 0)
         for i in range(4):
             turn_y(1, i)
         regroup(("Y", 1), y_t[1], 1)
-        for h in range(2):
-            quantize(("Y", 1), y_codes[1], y_sc[:, 1, :], h)
-        nc.sync.dma_start(out=out_1[1].rearrange("p m t -> p (m t)").bitcast(I32), in_=y_codes[1][:])
+        store_planes(1)
         for Q in range(4):
             nc.scalar.dma_start(out=out_2[:, 4 * Q:4 * Q + 4, :].rearrange("g r n -> r g n").bitcast(I32),
                                 in_=y_sc[32 * Q:32 * Q + 4, :, :].bitcast(I32))

@@ -16,8 +16,14 @@ ALU = mybir.AluOpType
 ACT = mybir.ActivationFunctionType
 
 P = 128
-W = 512
-SHARED = {("D", 1): "handed_d", ("D", 2): "handed_d"}
+SLOTS = 4
+GROUP = P * SLOTS
+HALF = GROUP // 2
+ROTATING_BANKS = 4
+STAGED_TILES = 4
+GROUPED_TILES = 4
+GPSIMD_TERMS = 3
+ROW_TILES = 8
 
 
 def tile_ancestry_adjusted_polygenic_scores_k4_kernel(
@@ -35,11 +41,23 @@ def tile_ancestry_adjusted_polygenic_scores_k4_kernel(
         def kept(name, shape, dtype):
             return keep.tile(shape, dtype, name=name, align_bytes=64)
 
-        def rot_bank(name, shape):
-            return psum.tile(shape, F32, name=name, tag="rot", bufs=4)
+        def rotating_bank(name, shape):
+            return psum.tile(shape, F32, name=name, tag="rotating", bufs=ROTATING_BANKS)
 
-        def acc_bank(name, j, shape):
-            return psum.tile(shape, F32, name=name, tag="acc%d" % j, bufs=1)
+        def score_bank(name, j, shape):
+            return psum.tile(shape, F32, name=name, tag="score%d" % j, bufs=1)
+
+        def half_cols(h):
+            return slice(HALF * h, HALF * (h + 1))
+
+        def tile_cols(i):
+            return slice(P * i, P * (i + 1))
+
+        def label(key):
+            return "".join(str(part) for part in key)
+
+        dosage = [("D", G) for G in range(4)]
+        effect = [[("B", g, G) for G in range(4)] for g in range(2)]
 
         h_words = impute_words.bitcast(I32)
         h_scales = impute_scales.bitcast(I32)
@@ -48,488 +66,430 @@ def tile_ancestry_adjusted_polygenic_scores_k4_kernel(
 
         ident = kept("ident", [P, P], F32)
         x_raw = [kept("x_raw%d" % i, [P, 2, K], BF16) for i in range(2)]
-        h_raw = [kept("h_raw%d" % G, [P, 2, 256], I32) for G in range(4)]
-        l_raw = [kept("l_raw%d" % G, [P, W], I32) for G in range(4)]
-        c_raw = [[kept("c_raw%d%d" % (g, h), [P, 4, 256], BF16) for h in range(2)] for g in range(1)] + [kept("c_raw1", [P, 4, W], BF16)]
-        hs_raw = kept("hs_raw", [P, 2, W], I32)
-        ls_raw = kept("ls_raw", [P, P], I32)
-        v_rows = kept("v_rows", [4, W], BF16)
-        v_sorted = kept("v_sorted", [P, 4, P], F32)
-        v_cols = kept("v_cols", [P, 4, 4], F32)
-        d_rows = kept("d_rows", [4, W], BF16)
-        d_sorted = kept("d_sorted", [P, 4, P], F32)
-        d_cols = kept("d_cols", [P, 4, 4], F32)
-        slope_col = kept("slope_col", [P, 2, 4], BF16)
-        icpt_col = kept("icpt_col", [P, 2, 4], BF16)
-        ts_col = kept("ts_col", [P, 2, 4], BF16)
-        anc_raw = kept("anc_raw", [P, 4], BF16)
-        anc_col = kept("anc_col", [P, 4], F32)
-        anc_all = kept("anc_all", [P, N], F32)
-        ab_col = kept("ab_col", [P, 2, 8], F32)
-        h_st = [kept("h_st%d" % G, [P, 2, 1024], U8) for G in range(4)]
-        hs_st = [kept("hs_st%d" % G, [P, 2, W], U8) for G in range(4)]
-        l_st = [kept("l_st%d" % G, [P, W], I32) for G in range(4)]
-        ls_st = kept("ls_st", [P, W], U8)
-        x_t = kept("x_t", [P, 2, N, 2], F32)
+        h_raw = [kept("h_raw%d" % G, [P, 2, GROUP // 2], I32) for G in range(4)]
+        l_raw = [kept("l_raw%d" % G, [P, GROUP], I32) for G in range(4)]
+        c_first = [kept("c_first%d" % h, [P, SLOTS, HALF], BF16) for h in range(2)]
+        c_second = kept("c_second", [P, SLOTS, GROUP], BF16)
+        hs_raw = kept("hs_raw", [P, 2, V // 4], I32)
+        ls_raw = kept("ls_raw", [P, GROUP // 4], I32)
+        factor_rows = kept("factor_rows", [8, GROUP], BF16)
+        factor_sorted = kept("factor_sorted", [P, SLOTS, P], F32)
+        factors = kept("factors", [P, 8, SLOTS], F32)
+        slope_col = kept("slope_col", [P, 2, SLOTS], BF16)
+        intercept_col = kept("intercept_col", [P, 2, SLOTS], BF16)
+        scale_col = kept("scale_col", [P, 2, SLOTS], BF16)
+        ancestry_all = kept("ancestry_all", [P, N], BF16)
+        line_col = kept("line_col", [P, 2, 2 * SLOTS], F32)
+        h_sorted = [kept("h_sorted%d" % G, [P, 2, 2 * GROUP], U8) for G in range(4)]
+        hs_sorted = [kept("hs_sorted%d" % G, [P, 2, GROUP], U8) for G in range(4)]
+        l_sorted = [kept("l_sorted%d" % G, [P, GROUP], I32) for G in range(4)]
+        ls_sorted = kept("ls_sorted", [P, GROUP], U8)
+        x_turned = kept("x_turned", [P, 2, N, 2], F32)
         x_codes = [kept("x_codes%d" % g, [P, N], I32) for g in range(2)]
-        x_sc = [kept("x_sc%d" % g, [P, N], U8) for g in range(2)]
-        c_codes = [kept("c_codes%d" % g, [P, W], I32) for g in range(2)]
-        c_sc = [kept("c_sc%d" % g, [P, W], U8) for g in range(2)]
-        keys = [("D", G) for G in range(4)] + [("B", g, G) for g in range(2) for G in range(4)]
+        x_scales = [kept("x_scales%d" % g, [P, N], U8) for g in range(2)]
+        c_codes = [kept("c_codes%d" % g, [P, GROUP], I32) for g in range(2)]
+        c_scales = [kept("c_scales%d" % g, [P, GROUP], U8) for g in range(2)]
         codes = {}
         scales = {}
-        for key in keys:
-            label = "".join(str(s) for s in key)
-            codes[key] = [kept("codes%s_%d" % (label, h), [P, 256], I32) for h in range(2)] if key[0] == "B" else kept("codes%s" % label, [P, W], I32)
-            scales[key] = [kept("scales%s_%d" % (label, h), [P, 256], U8) for h in range(2)] if key[0] == "B" else kept("scales%s" % label, [P, W], U8)
-        y_t = [kept("y_t%d" % g, [P, 4, N], F32) for g in range(2)]
+        for key in dosage:
+            codes[key] = kept("codes%s" % label(key), [P, N], I32)
+            scales[key] = kept("scales%s" % label(key), [P, N], U8)
+        for key in effect[0] + effect[1]:
+            codes[key] = [kept("codes%s_%d" % (label(key), h), [P, HALF], I32) for h in range(2)]
+            scales[key] = [kept("scales%s_%d" % (label(key), h), [P, HALF], U8) for h in range(2)]
+        y_turned = [kept("y_turned%d" % g, [P, SLOTS, N], F32) for g in range(2)]
         y_codes = [kept("y_codes%d" % g, [P, N], I32) for g in range(2)]
-        y_sc = kept("y_sc", [P, 2, N], U8)
+        y_scales = kept("y_scales", [P, 2, N], U8)
 
         make_identity(nc, ident[:])
-        nc.vector.memset(v_sorted[:], 0.0)
+        nc.vector.memset(factor_sorted[:, 0, :], 0.0)
         nc.vector.memset(ls_raw[:], 0)
         nc.vector.memset(hs_raw[:], 0)
-        nc.scalar.activation(out=d_sorted[:], in_=v_sorted[:], func=ACT.Copy)
+        nc.scalar.activation(out=factor_sorted[:, 1:SLOTS, :],
+                             in_=factor_sorted[:, 0:1, :].to_broadcast([P, SLOTS - 1, P]), func=ACT.Copy)
 
         def load_x(i):
-            nc.sync.dma_start(out=x_raw[i][:], in_=x[256 * i:256 * (i + 1), :].rearrange("(i p) k -> p i k", p=P))
+            nc.sync.dma_start(out=x_raw[i][:], in_=x[2 * P * i:2 * P * (i + 1), :].rearrange("(i p) k -> p i k", p=P))
 
         def load_h(G):
-            nc.sync.dma_start(out=h_raw[G][:], in_=h_words[:, :, 256 * G:256 * (G + 1)].rearrange("g p c -> p g c"))
+            nc.sync.dma_start(out=h_raw[G][:], in_=h_words[:, :, half_cols(G)].rearrange("g p c -> p g c"))
 
         def load_l(G):
-            nc.sync.dma_start(out=l_raw[G][:], in_=l_words[:, W * G:W * (G + 1)])
+            nc.sync.dma_start(out=l_raw[G][:], in_=l_words[:, GROUP * G:GROUP * (G + 1)])
 
-        def load_c(g):
-            nc.sync.dma_start(out=c_raw[g][:], in_=trait_factors[:, W * g:W * (g + 1)].rearrange("(p f) c -> p f c", f=4))
+        def load_c(target, cols):
+            nc.sync.dma_start(out=target[:], in_=trait_factors[:, cols].rearrange("(p f) c -> p f c", f=SLOTS))
 
-        def load_c_half(h):
-            nc.sync.dma_start(out=c_raw[0][h][:], in_=trait_factors[:, 256 * h:256 * (h + 1)].rearrange("(p f) c -> p f c", f=4))
-
-        def load_rows(first, rows, vector):
-            nc.sync.dma_start(out=d_rows[first:first + rows, :], in_=vector.rearrange("(g c) -> g c", g=rows))
-
-        def load_l_scales():
-            for Q in range(4):
-                nc.sync.dma_start(out=ls_raw[32 * Q:32 * Q + 16, :], in_=l_scales[4 * Q:4 * Q + 4, :].rearrange("r (G c) -> G r c", G=4))
-
-        def load_h_scales():
-            for Q in range(4):
-                nc.sync.dma_start(out=hs_raw[32 * Q:32 * Q + 4, :, :], in_=h_scales[:, 4 * Q:4 * Q + 4, :].rearrange("g r c -> r g c"))
-
-        def load_trait_columns():
-            nc.sync.dma_start(out=anc_raw[:], in_=ancestry.rearrange("(p j) -> p j", j=4))
-            for tile_, vector in ((ts_col, trait_scale), (slope_col, slope), (icpt_col, intercept)):
-                nc.sync.dma_start(out=tile_[:], in_=vector.rearrange("(g p j) -> p g j", g=2, j=4))
-
-        nc.sync.dma_start(out=v_rows[:], in_=variant_weight.rearrange("(G c) -> G c", G=4))
-        load_c_half(0)
+        for first, vector in ((0, variant_weight), (4, dosage_scale)):
+            nc.sync.dma_start(out=factor_rows[first:first + 4, :], in_=vector.rearrange("(G c) -> G c", G=4))
+        load_c(c_first[0], half_cols(0))
         load_l(0)
-        load_l_scales()
-        load_c_half(1)
+        for Q in range(4):
+            nc.sync.dma_start(out=ls_raw[32 * Q:32 * Q + 16, :],
+                              in_=l_scales[4 * Q:4 * Q + 4, :].rearrange("r (G c) -> G r c", G=4))
+        load_c(c_first[1], half_cols(1))
         load_l(1)
         load_x(0)
         load_x(1)
-        load_h_scales()
+        for r in range(4):
+            nc.sync.dma_start(out=hs_raw[r:P:32, :, :], in_=h_scales[:, r:16:4, :].rearrange("g Q c -> Q g c"))
         load_l(2)
         load_h(0)
-        load_rows(0, 4, dosage_scale)
         load_h(1)
         load_l(3)
-        load_c(1)
+        load_c(c_second, slice(GROUP, T))
         load_h(2)
-        load_trait_columns()
+        for column, vector in ((scale_col, trait_scale), (slope_col, slope), (intercept_col, intercept)):
+            nc.sync.dma_start(out=column[:], in_=vector.rearrange("(g p j) -> p g j", g=2, j=SLOTS))
         load_h(3)
+        nc.sync.dma_start(out=ancestry_all[:], in_=ancestry.partition_broadcast(P))
 
         def sort_h(G):
             nc.vector.tensor_copy(
-                out=h_st[G][:].bitcast(I32).rearrange("p g (t q r) -> p g t q r", t=4, q=16),
-                in_=h_raw[G][:].rearrange("p g (q t r) -> p g t q r", t=4, q=16))
+                out=h_sorted[G][:].bitcast(I32).rearrange("p g (t q r) -> p g t q r", t=SLOTS, q=16),
+                in_=h_raw[G][:].rearrange("p g (q t r) -> p g t q r", t=SLOTS, q=16))
             nc.vector.tensor_copy(
-                out=hs_st[G][:].bitcast(I32).rearrange("p g (t q r) -> p g t q r", t=4, q=16),
-                in_=hs_raw[:, :, P * G:P * (G + 1)].rearrange("p g (q t r) -> p g t q r", t=4, q=16))
+                out=hs_sorted[G][:].bitcast(I32).rearrange("p g (t q r) -> p g t q r", t=SLOTS, q=16),
+                in_=hs_raw[:, :, tile_cols(G)].rearrange("p g (q t r) -> p g t q r", t=SLOTS, q=16))
 
         def sort_l(G):
             nc.vector.tensor_copy(
-                out=l_st[G][:].rearrange("p (t q r) -> p t q r", t=4, q=16),
-                in_=l_raw[G][:].rearrange("p (q t r) -> p t q r", t=4, q=16))
+                out=l_sorted[G][:].rearrange("p (t q r) -> p t q r", t=SLOTS, q=16),
+                in_=l_raw[G][:].rearrange("p (q t r) -> p t q r", t=SLOTS, q=16))
 
         def sort_l_scales():
             nc.vector.tensor_copy(
-                out=ls_st[:].bitcast(I32).rearrange("p (t q r) -> p t q r", t=4, q=16),
-                in_=ls_raw[:].rearrange("p (q t r) -> p t q r", t=4, q=16))
+                out=ls_sorted[:].bitcast(I32).rearrange("p (t q r) -> p t q r", t=SLOTS, q=16),
+                in_=ls_raw[:].rearrange("p (q t r) -> p t q r", t=SLOTS, q=16))
 
-        x_banks = {}
+        def spread_factors():
+            nc.vector.tensor_copy(out=factor_sorted[0:8, :, :].rearrange("p t (q r) -> p t q r", r=8),
+                                  in_=factor_rows[:].rearrange("p (q t r) -> p t q r", t=SLOTS, r=8))
+            bank = rotating_bank("factor_bank", [P, SLOTS, P])
+            for t in range(SLOTS):
+                nc.tensor.transpose(bank[:, t, :], factor_sorted[:, t, :], ident[:])
+            nc.scalar.copy(out=factors[:], in_=bank[:, :, 0:8].rearrange("p t row -> p row t"))
 
         def turn_x(i):
             words = x_raw[i // 2][:, i % 2, :].bitcast(F32)
-            x_banks[i] = acc_bank("x_bank%d" % i, i, [P, 2, 2, P])
+            bank = score_bank("x_bank%d" % i, i, [P, 2, 2, P])
             for g in range(2):
                 for u in range(2):
-                    nc.tensor.transpose(x_banks[i][:, g, u, :], words[:, 256 * g + u:256 * (g + 1):2], ident[:])
-
-        def gather_x(i):
-            nc.scalar.copy(out=x_t[:, :, P * i:P * (i + 1), :], in_=x_banks[i][:].rearrange("p g u r -> p g r u"))
+                    nc.tensor.transpose(bank[:, g, u, :], words[:, HALF * g + u:HALF * (g + 1):2], ident[:])
+            nc.scalar.copy(out=x_turned[:, :, tile_cols(i), :], in_=bank[:].rearrange("p g u n -> p g n u"))
 
         def quantize_x(g):
-            nc.vector.quantize_mx(out=x_codes[g][:].bitcast(FP8X4), scales=x_sc[g][:],
-                                  in_=x_t[:, g, :, :].rearrange("p n u -> p (n u)").bitcast(BF16))
-
-        c_grouped = {}
-
-        def prepare_c_interleave(g, on_scalar, h):
-            if h == 0:
-                c_grouped[g] = flow.tile([P, W, 4], BF16, name="c_grouped%d" % g, tag="grouped", bufs=4, align_bytes=64)
-            if True:
-                (nc.scalar.copy if on_scalar else nc.vector.tensor_copy)(
-                    out=c_grouped[g][:, 256 * h:256 * (h + 1), :].rearrange("p (j m) f -> p j m f", j=2),
-                    in_=c_raw[g][:].rearrange("p f (m j) -> p j m f", j=4)[:, 2 * h:2 * h + 2, :, :])
-
-        def prepare_c_quantize(g):
-            for h in range(2):
-                nc.vector.quantize_mx(out=c_codes[g][:, 256 * h:256 * (h + 1)].bitcast(FP8X4), scales=c_sc[g][:, 256 * h:256 * (h + 1)],
-                                      in_=c_grouped[g][:, 256 * h:256 * (h + 1), :].rearrange("p c f -> p (c f)"))
-
-        def prepare_c_half(h):
-            if h == 0:
-                c_grouped[0] = flow.tile([P, W, 4], BF16, name="c_grouped0", tag="grouped", bufs=4, align_bytes=64)
-            nc.vector.tensor_copy(out=c_grouped[0][:, 256 * h:256 * (h + 1), :].rearrange("p (j m) f -> p j m f", j=4),
-                                  in_=c_raw[0][h][:].rearrange("p f (m j) -> p j m f", j=4))
-
-        def quantize_c_half(h):
-            nc.vector.quantize_mx(out=c_codes[0][:, 256 * h:256 * (h + 1)].bitcast(FP8X4), scales=c_sc[0][:, 256 * h:256 * (h + 1)],
-                                  in_=c_grouped[0][:, 256 * h:256 * (h + 1), :].rearrange("p c f -> p (c f)"))
-
-        def sort_variant_rows(rows, in_order):
-            nc.vector.tensor_copy(out=in_order[0:4, :, :].rearrange("p t (q r) -> p t q r", r=8),
-                                  in_=rows[0:4, :].rearrange("p (q t r) -> p t q r", t=4, r=8))
-
-        def turn_rows(in_order, name):
-            bank = rot_bank(name, [P, 4, P])
-            for t in range(4):
-                nc.tensor.transpose(bank[:, t, :], in_order[:, t, :], ident[:])
-            return bank
-
-        staged = {}
-
-        def label(key):
-            return "".join(str(part) for part in key)
-
-        def first_stage(key, t):
-            G = key[-1]
-            bank = rot_bank("bank_%s%d" % (label(key), t), [P, W])
-            if key[0] == "D":
-                for g in range(2):
-                    nc.tensor.matmul_mx(out=bank[:], lhsT=h_st[G][:, g, 256 * t:256 * (t + 1)].bitcast(FP4X4),
-                                        lhsT_scale=hs_st[G][:, g, P * t:P * (t + 1)],
-                                        rhs=x_codes[g][:].bitcast(FP8X4), rhs_scale=x_sc[g][:],
-                                        start=(g == 0), stop=(g == 1))
-                factor = d_cols[:, G, t:t + 1]
-            else:
-                g = key[1]
-                nc.tensor.matmul_mx(out=bank[:], lhsT=l_st[G][:, P * t:P * (t + 1)].bitcast(FP8X4),
-                                    lhsT_scale=ls_st[4 * G:, P * t:P * (t + 1)],
-                                    rhs=c_codes[g][:].bitcast(FP8X4), rhs_scale=c_sc[g][:],
-                                    start=True, stop=True)
-                factor = v_cols[:, G, t:t + 1]
-            if t == 0:
-                staged[key] = flow.tile([P, 4, W], BF16, name="staged_%s" % label(key), tag="staged", bufs=4, align_bytes=64)
-            if key[:2] == ("B", 0):
-                nc.scalar.activation(out=staged[key][:, t, :].rearrange("p (j h m) -> p h j m", j=4, h=2),
-                                     in_=bank[:].rearrange("p (h j m) -> p h j m", j=4, h=2), func=ACT.Copy, scale=factor)
-            else:
-                nc.scalar.activation(out=staged[key][:, t, :], in_=bank[:], func=ACT.Copy, scale=factor)
-
-        def first_stage_half(G, h, g=1):
-            cols = slice(256 * h, 256 * (h + 1))
-            if h == 0:
-                staged["B", g, G] = flow.tile([P, 4, W], BF16, name="staged_B%d%d" % (g, G), tag="staged", bufs=4, align_bytes=64)
-            for pair in range(2):
-                bank = rot_bank("bank_B%d%d_%d%d" % (g, G, h, pair), [P, 2, 256])
-                for u in range(2):
-                    t = 2 * pair + u
-                    nc.tensor.matmul_mx(out=bank[:, u, :], lhsT=l_st[G][:, P * t:P * (t + 1)].bitcast(FP8X4),
-                                        lhsT_scale=ls_st[4 * G:, P * t:P * (t + 1)],
-                                        rhs=c_codes[g][:, cols].bitcast(FP8X4), rhs_scale=c_sc[g][:, cols],
-                                        start=True, stop=True)
-                for u in range(2):
-                    t = 2 * pair + u
-                    if g == 0:
-                        nc.scalar.activation(out=staged["B", g, G][:, t, :].rearrange("p (j h m) -> p h j m", j=4, h=2)[:, h, :, :],
-                                             in_=bank[:, u, :].rearrange("p (j m) -> p j m", j=4), func=ACT.Copy, scale=v_cols[:, G, t:t + 1])
-                    else:
-                        nc.scalar.activation(out=staged["B", g, G][:, t, cols], in_=bank[:, u, :], func=ACT.Copy, scale=v_cols[:, G, t:t + 1])
-
-        def interleave(dst, src, h, on_scalar=False):
-            (nc.scalar.copy if on_scalar else nc.vector.tensor_copy)(
-                out=dst[:, 256 * h:256 * (h + 1), :].rearrange("p (c i) t -> p c t i", i=4),
-                in_=src[:, :, 256 * h:256 * (h + 1)].rearrange("p t (c i) -> p c t i", i=4))
-
-        def half(tiles, h):
-            return tiles[h][:] if isinstance(tiles, list) else tiles[:, 256 * h:256 * (h + 1)]
+            nc.vector.quantize_mx(out=x_codes[g][:].bitcast(FP8X4), scales=x_scales[g][:],
+                                  in_=x_turned[:, g, :, :].rearrange("p n u -> p (n u)").bitcast(BF16))
 
         grouped = {}
 
-        def regroup(key, src, h, on_scalar=False):
+        def grouped_tile(key):
             if key not in grouped:
-                if key in SHARED:
-                    grouped[key] = flow.tile([P, W, 4], BF16, name="grouped_%s" % label(key), tag=SHARED[key], bufs=1, align_bytes=64)
+                if key in dosage[1:3]:
+                    grouped[key] = flow.tile([P, GROUP, SLOTS], BF16, name="grouped_%s" % label(key),
+                                             tag="handed_on", bufs=1, align_bytes=64)
                 else:
-                    grouped[key] = flow.tile([P, W, 4], BF16, name="grouped_%s" % label(key), tag="grouped", bufs=4, align_bytes=64)
-            if on_scalar == "G":
-                cols = slice(256 * h, 256 * (h + 1))
-                nc.gpsimd.tensor_scalar(out=grouped[key][:, cols, :], in0=src[:, :, cols].rearrange("p t c -> p c t"),
-                                        scalar1=1.0, scalar2=0.0, op0=ALU.mult, op1=ALU.add)
+                    grouped[key] = flow.tile([P, GROUP, SLOTS], BF16, name="grouped_%s" % label(key),
+                                             tag="grouped", bufs=GROUPED_TILES, align_bytes=64)
+            return grouped[key]
+
+        def quantize(key, h, out_codes, out_scales):
+            nc.vector.quantize_mx(out=out_codes.bitcast(FP8X4), scales=out_scales,
+                                  in_=grouped[key][:, half_cols(h), :].rearrange("p c t -> p (c t)"))
+
+        def group_c_first(h):
+            nc.vector.tensor_copy(
+                out=grouped_tile(("C", 0))[:, half_cols(h), :].rearrange("p (j m) f -> p j m f", j=SLOTS),
+                in_=c_first[h][:].rearrange("p f (m j) -> p j m f", j=SLOTS))
+
+        def group_c_second(h):
+            nc.scalar.copy(
+                out=grouped_tile(("C", 1))[:, half_cols(h), :].rearrange("p (j m) f -> p j m f", j=2),
+                in_=c_second[:].rearrange("p f (m j) -> p j m f", j=SLOTS)[:, 2 * h:2 * h + 2, :, :])
+
+        def quantize_c(g, h):
+            quantize(("C", g), h, c_codes[g][:, half_cols(h)], c_scales[g][:, half_cols(h)])
+
+        staged = {}
+
+        def staged_tile(key):
+            if key not in staged:
+                staged[key] = flow.tile([P, SLOTS, GROUP], BF16, name="staged_%s" % label(key),
+                                        tag="staged", bufs=STAGED_TILES, align_bytes=64)
+            return staged[key]
+
+        def effect_matmul(out, g, G, t, cols):
+            nc.tensor.matmul_mx(out=out, lhsT=l_sorted[G][:, tile_cols(t)].bitcast(FP8X4),
+                                lhsT_scale=ls_sorted[4 * G:, tile_cols(t)],
+                                rhs=c_codes[g][:, cols].bitcast(FP8X4), rhs_scale=c_scales[g][:, cols],
+                                start=True, stop=True)
+
+        def joined(ap):
+            return ap.rearrange("p (j h m) -> p h j m", j=SLOTS, h=2)
+
+        def stage_dosage(G, t):
+            bank = rotating_bank("bank_D%d%d" % (G, t), [P, N])
+            for g in range(2):
+                nc.tensor.matmul_mx(out=bank[:], lhsT=h_sorted[G][:, g, half_cols(t)].bitcast(FP4X4),
+                                    lhsT_scale=hs_sorted[G][:, g, tile_cols(t)],
+                                    rhs=x_codes[g][:].bitcast(FP8X4), rhs_scale=x_scales[g][:],
+                                    start=(g == 0), stop=(g == 1))
+            nc.scalar.activation(out=staged_tile(dosage[G])[:, t, :], in_=bank[:], func=ACT.Copy,
+                                 scale=factors[:, 4 + G, t:t + 1])
+
+        def stage_effect(g, G, t):
+            bank = rotating_bank("bank_B%d%d%d" % (g, G, t), [P, GROUP])
+            effect_matmul(bank[:], g, G, t, slice(0, GROUP))
+            out, in_ = staged_tile(effect[g][G])[:, t, :], bank[:]
+            if g == 0:
+                out, in_ = joined(out), in_.rearrange("p (h j m) -> p h j m", j=SLOTS, h=2)
+            nc.scalar.activation(out=out, in_=in_, func=ACT.Copy, scale=factors[:, G, t:t + 1])
+
+        def stage_effect_half(g, G, h):
+            target = staged_tile(effect[g][G])
+            for pair in range(2):
+                bank = rotating_bank("bank_B%d%d_%d%d" % (g, G, h, pair), [P, 2, HALF])
+                for u in range(2):
+                    effect_matmul(bank[:, u, :], g, G, 2 * pair + u, half_cols(h))
+                for u in range(2):
+                    t = 2 * pair + u
+                    if g == 0:
+                        out, in_ = joined(target[:, t, :])[:, h, :, :], bank[:, u, :].rearrange("p (j m) -> p j m", j=SLOTS)
+                    else:
+                        out, in_ = target[:, t, half_cols(h)], bank[:, u, :]
+                    nc.scalar.activation(out=out, in_=in_, func=ACT.Copy, scale=factors[:, G, t:t + 1])
+
+        def direct_effect(g, G, c, bank):
+            for t in range(SLOTS):
+                effect_matmul(bank[:, t, :], g, G, t, tile_cols(c))
+            target = grouped_tile(effect[g][G])
+            if g == 0:
+                pair = slice(2 * (c % 2), 2 * (c % 2) + 2)
+                out = target[:].rearrange("p (j h m) t -> p h j m t", j=SLOTS, h=2)[:, c // 2, pair, :, :]
+                in0 = bank[:].rearrange("p t (j m) -> p j m t", j=2)
+                in1 = factors[:, G, :].unsqueeze(1).unsqueeze(1).to_broadcast([P, 2, P // 2, SLOTS])
             else:
-                interleave(grouped[key], src, h, on_scalar)
+                out = target[:, tile_cols(c), :]
+                in0 = bank[:].rearrange("p t n -> p n t")
+                in1 = factors[:, G, :].unsqueeze(1).to_broadcast([P, P, SLOTS])
+            nc.vector.tensor_tensor(out=out, in0=in0, in1=in1, op=ALU.mult)
 
-        def quantize(key, dst_codes, dst_scales, h):
-            nc.vector.quantize_mx(out=half(dst_codes, h).bitcast(FP8X4), scales=half(dst_scales, h),
-                                  in_=grouped[key][:, 256 * h:256 * (h + 1), :].rearrange("p c t -> p (c t)"))
+        def direct_in_rotation(g, G, c):
+            direct_effect(g, G, c, rotating_bank("bank_B%d%d%d" % (g, G, c), [P, SLOTS, P]))
 
-        def finish_group(key):
-            for h in range(2):
-                regroup(key, staged[key], h)
-            for h in range(2):
-                quantize(key, codes[key], scales[key], h)
+        def direct_in_score_bank(g, G, c, j):
+            direct_effect(g, G, c, score_bank("bank_B%d%d%d" % (g, G, c), j, [P, SLOTS, P]))
 
-        def direct(key, c, acc_slot=None):
-            g, G = key[1], key[2]
-            cols = slice(P * c, P * (c + 1))
-            if acc_slot is not None:
-                bank = acc_bank("bank_%s%d" % (label(key), c), acc_slot, [P, 4, P])
+        def interleave(copy, key, source, h):
+            copy(out=grouped_tile(key)[:, half_cols(h), :].rearrange("p (c i) t -> p c t i", i=4),
+                 in_=source[:, :, half_cols(h)].rearrange("p t (c i) -> p c t i", i=4))
+
+        def regroup(key, h):
+            interleave(nc.vector.tensor_copy, key, staged[key], h)
+
+        def regroup_on_gpsimd(key, h):
+            nc.gpsimd.tensor_scalar(out=grouped_tile(key)[:, half_cols(h), :],
+                                    in0=staged[key][:, :, half_cols(h)].rearrange("p t c -> p c t"),
+                                    scalar1=1.0, scalar2=0.0, op0=ALU.mult, op1=ALU.add)
+
+        def quantize_half(key, h):
+            if key in dosage:
+                quantize(key, h, codes[key][:, half_cols(h)], scales[key][:, half_cols(h)])
             else:
-                bank = rot_bank("bank_%s%d" % (label(key), c), [P, 4, P])
-            for t in range(4):
-                nc.tensor.matmul_mx(out=bank[:, t, :], lhsT=l_st[G][:, P * t:P * (t + 1)].bitcast(FP8X4),
-                                    lhsT_scale=ls_st[4 * G:, P * t:P * (t + 1)],
-                                    rhs=c_codes[g][:, cols].bitcast(FP8X4), rhs_scale=c_sc[g][:, cols],
-                                    start=True, stop=True)
-            if key not in grouped:
-                grouped[key] = flow.tile([P, W, 4], BF16, name="grouped_%s" % label(key), tag="grouped", bufs=4, align_bytes=64)
-            if g == 1:
-                nc.vector.tensor_tensor(out=grouped[key][:, cols, :], in0=bank[:].rearrange("p t n -> p n t"),
-                                        in1=v_cols[:, G, :].unsqueeze(1).to_broadcast([P, P, 4]), op=ALU.mult)
-                return
-            nc.vector.tensor_tensor(out=grouped[key][:].rearrange("p (j h m) t -> p h j m t", j=4, h=2)[:, c // 2, 2 * (c % 2):2 * (c % 2) + 2, :, :],
-                                    in0=bank[:].rearrange("p t (j m) -> p j m t", j=2),
-                                    in1=v_cols[:, G, :].unsqueeze(1).unsqueeze(1).to_broadcast([P, 2, 64, 4]), op=ALU.mult)
+                quantize(key, h, codes[key][h][:], scales[key][h][:])
 
         def quantize_group(key):
             for h in range(2):
-                quantize(key, codes[key], scales[key], h)
+                quantize_half(key, h)
 
-        acc = {}
+        def finish_group(key):
+            for h in range(2):
+                regroup(key, h)
+            quantize_group(key)
+
+        score = {}
 
         def second_stage(g, G, j):
             if G == 0:
-                acc[g, j] = acc_bank("acc%d_%d" % (g, j), j, [P, N])
-            cols = slice(P * (j % 2), P * (j % 2 + 1))
-            nc.tensor.matmul_mx(out=acc[g, j][:], lhsT=codes["B", g, G][j // 2][:, cols].bitcast(FP8X4),
-                                lhsT_scale=scales["B", g, G][j // 2][:, cols],
-                                rhs=codes["D", G][:].bitcast(FP8X4), rhs_scale=scales["D", G][:],
+                score[g, j] = score_bank("score%d_%d" % (g, j), j, [P, N])
+            key = effect[g][G]
+            nc.tensor.matmul_mx(out=score[g, j][:], lhsT=codes[key][j // 2][:, tile_cols(j % 2)].bitcast(FP8X4),
+                                lhsT_scale=scales[key][j // 2][:, tile_cols(j % 2)],
+                                rhs=codes[dosage[G]][:].bitcast(FP8X4), rhs_scale=scales[dosage[G]][:],
                                 start=(G == 0), stop=(G == 3))
 
-        expected = {}
+        def scale_lines():
+            for a, column in enumerate((slope_col, intercept_col)):
+                nc.vector.tensor_tensor(out=line_col[:, a, :], in0=column[:].rearrange("p g j -> p (g j)"),
+                                        in1=scale_col[:].rearrange("p g j -> p (g j)"), op=ALU.mult)
 
-        def make_expected(g, j, on_scalar):
-            c = 4 * g + j
-            if on_scalar:
-                expected[g, j] = kept("expected%d%d" % (g, j), [P, N], F32)
-            else:
-                expected[g, j] = flow.tile([P, N], F32, name="expected%d%d" % (g, j), tag="expected", bufs=3)
-            if on_scalar:
-                nc.scalar.activation(out=expected[g, j][:], in_=anc_all[:], func=ACT.Identity,
-                                     scale=ab_col[:, 0, c:c + 1], bias=ab_col[:, 1, c:c + 1])
-            else:
-                nc.gpsimd.tensor_scalar(out=expected[g, j][:], in0=anc_all[:], scalar1=ab_col[:, 0, c:c + 1],
-                                        scalar2=ab_col[:, 1, c:c + 1], op0=ALU.mult, op1=ALU.add)
+        term = {}
+
+        def ancestry_term_on_gpsimd(g, j):
+            c = SLOTS * g + j
+            term[g, j] = flow.tile([P, N], F32, name="term%d%d" % (g, j), tag="term", bufs=GPSIMD_TERMS)
+            nc.gpsimd.tensor_scalar(out=term[g, j][:], in0=ancestry_all[:], scalar1=line_col[:, 0, c:c + 1],
+                                    scalar2=line_col[:, 1, c:c + 1], op0=ALU.mult, op1=ALU.add)
+
+        def ancestry_term_on_scalar(g, j):
+            c = SLOTS * g + j
+            term[g, j] = kept("term%d%d" % (g, j), [P, N], F32)
+            nc.scalar.activation(out=term[g, j][:], in_=ancestry_all[:], func=ACT.Identity,
+                                 scale=line_col[:, 0, c:c + 1], bias=line_col[:, 1, c:c + 1])
 
         def adjust(g, j, cols):
-            nc.vector.scalar_tensor_tensor(out=y_t[g][:, j, cols], in0=acc[g, j][:, cols], scalar=ts_col[:, g, j:j + 1],
-                                           in1=expected[g, j][:, cols], op0=ALU.mult, op1=ALU.subtract)
+            nc.vector.scalar_tensor_tensor(out=y_turned[g][:, j, cols], in0=score[g, j][:, cols],
+                                           scalar=scale_col[:, g, j:j + 1], in1=term[g, j][:, cols],
+                                           op0=ALU.mult, op1=ALU.subtract)
 
-        def planes(g):
+        def round_y(copy, g, h):
+            interleave(copy, ("Y", g), y_turned[g], h)
+
+        def store_codes(g):
             for h in range(2):
-                regroup(("Y", g), y_t[g], h)
-            for h in range(2):
-                quantize(("Y", g), y_codes[g], y_sc[:, g, :], h)
+                quantize(("Y", g), h, y_codes[g][:, half_cols(h)], y_scales[:, g, half_cols(h)])
             nc.sync.dma_start(out=out_1[g].rearrange("p m t -> p (m t)").bitcast(I32), in_=y_codes[g][:])
 
-        def store_planes(g):
-            for h in range(2):
-                quantize(("Y", g), y_codes[g], y_sc[:, g, :], h)
-            nc.sync.dma_start(out=out_1[g].rearrange("p m t -> p (m t)").bitcast(I32), in_=y_codes[g][:])
-
-        def turn_y(g, i):
-            bank = rot_bank("y_bank%d_%d" % (g, i), [P, 4, P])
-            for j in range(4):
-                nc.tensor.transpose(bank[:, j, :], y_t[g][:, j, P * i:P * (i + 1)], ident[:])
-            rows = flow.tile([P, P, 4], F32, name="y_rows%d_%d" % (g, i), tag="y_rows", bufs=8)
+        def store_rows(g, i):
+            bank = rotating_bank("y_bank%d_%d" % (g, i), [P, SLOTS, P])
+            for j in range(SLOTS):
+                nc.tensor.transpose(bank[:, j, :], y_turned[g][:, j, tile_cols(i)], ident[:])
+            rows = flow.tile([P, P, SLOTS], F32, name="y_rows%d_%d" % (g, i), tag="y_rows", bufs=ROW_TILES)
             nc.scalar.copy(out=rows[:], in_=bank[:].rearrange("n j p -> n p j"))
-            nc.sync.dma_start(out=out_0[P * i:P * (i + 1), W * g:W * (g + 1)], in_=rows[:].rearrange("n p j -> n (p j)"))
+            nc.sync.dma_start(out=out_0[tile_cols(i), GROUP * g:GROUP * (g + 1)], in_=rows[:].rearrange("n p j -> n (p j)"))
 
-        everyone = slice(0, N)
-
-        def spread_ancestry():
-            anc_bank = rot_bank("anc_bank", [P, 4, P])
-            for j in range(4):
-                nc.tensor.transpose(anc_bank[:, j, :], anc_col[:, j:j + 1].to_broadcast([P, P]), ident[:])
-            nc.scalar.copy(out=anc_all[:].rearrange("p (r j) -> p r j", j=4), in_=anc_bank[:].rearrange("p j r -> p r j"))
-
-        def trait_products():
-            for a, vector in enumerate((slope_col, icpt_col)):
-                nc.vector.tensor_tensor(out=ab_col[:, a, :], in0=vector[:].rearrange("p g j -> p (g j)"),
-                                        in1=ts_col[:].rearrange("p g j -> p (g j)"), op=ALU.mult)
-
-        B = lambda g, G: ("B", g, G)
-        Dk = lambda G: ("D", G)
-        sort_variant_rows(v_rows, v_sorted)
-        v_bank = turn_rows(v_sorted, "v_bank")
-        nc.scalar.copy(out=v_cols[:], in_=v_bank[:, :, 0:4].rearrange("p t i -> p i t"))
-        prepare_c_half(0)
+        spread_factors()
+        group_c_first(0)
         sort_l(0)
-        quantize_c_half(0)
+        quantize_c(0, 0)
         sort_l_scales()
-        first_stage_half(0, 0, 0)
-        prepare_c_half(1)
+        stage_effect_half(0, 0, 0)
+        group_c_first(1)
         sort_l(1)
-        quantize_c_half(1)
-        direct(B(0, 1), 0, 2)
-        direct(B(0, 1), 1, 3)
-        first_stage_half(0, 1, 0)
-        direct(B(0, 1), 2)
-        direct(B(0, 1), 3)
+        quantize_c(0, 1)
+        for c in range(2):
+            direct_in_score_bank(0, 1, c, 2 + c)
+        stage_effect_half(0, 0, 1)
+        for c in range(2, 4):
+            direct_in_rotation(0, 1, c)
+
         for i in range(4):
             turn_x(i)
-            gather_x(i)
-        regroup(B(0, 0), staged[B(0, 0)], 0)
+        regroup(effect[0][0], 0)
         sort_l(2)
-        regroup(B(0, 0), staged[B(0, 0)], 1)
+        regroup(effect[0][0], 1)
         sort_h(0)
-        sort_variant_rows(d_rows, d_sorted)
-        for t in range(4):
-            first_stage(B(0, 2), t)
-        d_bank = turn_rows(d_sorted, "d_bank")
-        nc.scalar.copy(out=d_cols[:], in_=d_bank[:, :, 0:4].rearrange("p t i -> p i t"))
+        for t in range(SLOTS):
+            stage_effect(0, 2, t)
         quantize_x(0)
         quantize_x(1)
         sort_h(1)
-        quantize_group(B(0, 1))
+        quantize_group(effect[0][1])
         sort_l(3)
-        quantize_group(B(0, 0))
-        for t in range(4):
-            first_stage(Dk(0), t)
-        nc.vector.tensor_copy(out=anc_col[:], in_=anc_raw[:])
-        finish_group(B(0, 2))
+        quantize_group(effect[0][0])
+
+        for t in range(SLOTS):
+            stage_dosage(0, t)
+        finish_group(effect[0][2])
         sort_h(2)
         for t in range(2):
-            first_stage(Dk(1), t)
-        spread_ancestry()
-        finish_group(Dk(0))
-        trait_products()
-        for j in range(3):
-            make_expected(0, j, False)
-        prepare_c_interleave(1, True, 0)
-        first_stage(Dk(1), 2)
-        first_stage(Dk(1), 3)
-        prepare_c_interleave(1, True, 1)
-        for t in range(4):
-            direct(B(0, 3), t, t)
-        for t in range(4):
-            first_stage(Dk(2), t)
+            stage_dosage(1, t)
+        finish_group(dosage[0])
+        scale_lines()
+        for j in range(GPSIMD_TERMS):
+            ancestry_term_on_gpsimd(0, j)
+        group_c_second(0)
+        for t in range(2, SLOTS):
+            stage_dosage(1, t)
+        group_c_second(1)
+        for c in range(4):
+            direct_in_score_bank(0, 3, c, c)
+        for t in range(SLOTS):
+            stage_dosage(2, t)
         sort_h(3)
-        quantize_group(B(0, 3))
-        regroup(Dk(1), staged[Dk(1)], 0)
-        prepare_c_quantize(1)
-        regroup(Dk(1), staged[Dk(1)], 1)
-        second_stage(0, 0, 0)
-        first_stage(Dk(3), 0)
-        second_stage(0, 0, 1)
-        first_stage(Dk(3), 1)
-        make_expected(0, 3, True)
-        quantize_group(Dk(1))
-        regroup(Dk(2), staged[Dk(2)], 0, "G")
-        regroup(Dk(2), staged[Dk(2)], 1, "G")
-        direct(B(1, 0), 0)
-        direct(B(1, 0), 1)
-        first_stage(Dk(3), 2)
-        direct(B(1, 0), 2)
-        first_stage(Dk(3), 3)
-        direct(B(1, 0), 3)
-        regroup(Dk(3), staged[Dk(3)], 0, True)
-        second_stage(0, 0, 2)
-        second_stage(0, 0, 3)
-        quantize_group(Dk(2))
-        for t in range(4):
-            first_stage(B(1, 1), t)
+        quantize_group(effect[0][3])
+        regroup(dosage[1], 0)
+        for h in range(2):
+            quantize_c(1, h)
+        regroup(dosage[1], 1)
+        for t in range(2):
+            second_stage(0, 0, t)
+            stage_dosage(3, t)
+        ancestry_term_on_scalar(0, 3)
+        quantize_group(dosage[1])
+        for h in range(2):
+            regroup_on_gpsimd(dosage[2], h)
+        for c in range(2):
+            direct_in_rotation(1, 0, c)
+        for c in range(2, 4):
+            stage_dosage(3, c)
+            direct_in_rotation(1, 0, c)
+        interleave(nc.scalar.copy, dosage[3], staged[dosage[3]], 0)
+        for j in range(2, SLOTS):
+            second_stage(0, 0, j)
+        quantize_group(dosage[2])
+
+        for t in range(SLOTS):
+            stage_effect(1, 1, t)
             second_stage(0, 1, t)
-        regroup(Dk(3), staged[Dk(3)], 1)
-        quantize_group(Dk(3))
-        quantize_group(B(1, 0))
-        for t in range(4):
-            second_stage(0, 2, t)
-        regroup(B(1, 1), staged[B(1, 1)], 0)
-        for t in range(4):
-            second_stage(0, 3, t)
-        make_expected(1, 3, True)
-        first_stage_half(2, 0)
-        first_stage_half(3, 0)
-        b2, b3 = ("B", 1, 2), ("B", 1, 3)
-        for j in range(4):
-            adjust(0, j, everyone)
-            if j < 3:
-                make_expected(1, j, False)
-        regroup(B(1, 1), staged[B(1, 1)], 1)
-        second_stage(1, 0, 0)
-        second_stage(1, 0, 1)
-        first_stage_half(2, 1)
-        second_stage(1, 0, 2)
-        second_stage(1, 0, 3)
-        for i in range(0):
-            turn_y(0, i)
-        first_stage_half(3, 1)
-        regroup(b2, staged[b2], 0)
-        quantize_group(B(1, 1))
-        regroup(b3, staged[b3], 0)
-        quantize(b2, codes[b2], scales[b2], 0)
-        quantize(b3, codes[b3], scales[b3], 0)
-        for i in range(0, 2):
-            turn_y(0, i)
-        regroup(("Y", 0), y_t[0], 0, True)
-        for j in range(4):
+        regroup(dosage[3], 1)
+        quantize_group(dosage[3])
+        quantize_group(effect[1][0])
+        for j in range(SLOTS):
+            second_stage(0, 2, j)
+        regroup(effect[1][1], 0)
+        ancestry_term_on_scalar(1, 3)
+        stage_effect_half(1, 2, 0)
+        for j in range(SLOTS):
+            second_stage(0, 3, j)
+        stage_effect_half(1, 3, 0)
+        for j in range(SLOTS):
+            adjust(0, j, slice(0, N))
+            if j < GPSIMD_TERMS:
+                ancestry_term_on_gpsimd(1, j)
+        regroup(effect[1][1], 1)
+
+        for G in range(2, 4):
+            for j in range(2 * (G - 2), 2 * (G - 1)):
+                second_stage(1, 0, j)
+            stage_effect_half(1, G, 1)
+        regroup(effect[1][2], 0)
+        quantize_group(effect[1][1])
+        regroup(effect[1][3], 0)
+        for G in range(2, 4):
+            quantize_half(effect[1][G], 0)
+        for i in range(2):
+            store_rows(0, i)
+        round_y(nc.scalar.copy, 0, 0)
+        for j in range(SLOTS):
             second_stage(1, 1, j)
         for i in range(2, 4):
-            turn_y(0, i)
+            store_rows(0, i)
         for j in range(2):
-            second_stage(1, 2, j)
-            second_stage(1, 3, j)
-        regroup(b2, staged[b2], 1)
-        regroup(b3, staged[b3], 1)
-        quantize(b2, codes[b2], scales[b2], 1)
-        quantize(b3, codes[b3], scales[b3], 1)
+            for G in range(2, 4):
+                second_stage(1, G, j)
+        for G in range(2, 4):
+            regroup(effect[1][G], 1)
+        for G in range(2, 4):
+            quantize_half(effect[1][G], 1)
+        round_y(nc.scalar.copy, 0, 1)
+        for j in range(2):
+            adjust(1, j, slice(0, N))
+        for j in range(2, SLOTS):
+            for G in range(2, 4):
+                second_stage(1, G, j)
 
-        regroup(("Y", 0), y_t[0], 1, True)
-        adjust(1, 0, everyone)
-        adjust(1, 1, everyone)
-        for i in range(4, 4):
-            turn_y(0, i)
-        for j in range(2, 4):
-            second_stage(1, 2, j)
-            second_stage(1, 3, j)
-
-        for j in range(2, 4):
-            adjust(1, j, slice(0, 256))
-        store_planes(0)
-        for j in range(2, 4):
-            adjust(1, j, slice(256, 512))
-
-        regroup(("Y", 1), y_t[1], 0)
+        for j in range(2, SLOTS):
+            adjust(1, j, half_cols(0))
+        store_codes(0)
+        for j in range(2, SLOTS):
+            adjust(1, j, half_cols(1))
+        round_y(nc.vector.tensor_copy, 1, 0)
         for i in range(4):
-            turn_y(1, i)
-        regroup(("Y", 1), y_t[1], 1)
-        store_planes(1)
+            store_rows(1, i)
+        round_y(nc.vector.tensor_copy, 1, 1)
+        store_codes(1)
         for Q in range(4):
             nc.scalar.dma_start(out=out_2[:, 4 * Q:4 * Q + 4, :].rearrange("g r n -> r g n").bitcast(I32),
-                                in_=y_sc[32 * Q:32 * Q + 4, :, :].bitcast(I32))
+                                in_=y_scales[32 * Q:32 * Q + 4, :, :].bitcast(I32))

from contextlib import ExitStack

import concourse.mybir as mybir
from concourse.masks import make_identity

N, K, V, F, T = 512, 1024, 2048, 512, 1024
FLOPS = 2 * (N * K * V + V * F * T + N * V * T)

F32 = mybir.dt.float32
BF16 = mybir.dt.bfloat16
I32 = mybir.dt.int32
U8 = mybir.dt.uint8
FP8X4 = mybir.dt.float8_e4m3fn_x4
FP4X4 = mybir.dt.float4_e2m1fn_x4
ALU = mybir.AluOpType
ACT = mybir.ActivationFunctionType

P = 128
SLOTS = 4
GROUP = P * SLOTS
HALF = GROUP // 2
ROTATING_BANKS = 4
STAGED_TILES = 4
GROUPED_TILES = 4
GPSIMD_TERMS = 3
ROW_TILES = 8


def tile_ancestry_adjusted_polygenic_scores_k4_kernel(
    tc, x, impute_words, impute_scales, load_words, load_scales, trait_factors,
    dosage_scale, variant_weight, ancestry, slope, intercept, trait_scale,
    out_0, out_1, out_2,
):
    nc = tc.nc
    with ExitStack() as ctx:
        keep = ctx.enter_context(tc.tile_pool(name="keep", bufs=1))
        flow = ctx.enter_context(tc.tile_pool(name="flow", bufs=1))
        psum = ctx.enter_context(tc.psum_pool(name="psum", bufs=1))
        ctx.enter_context(tc.manual_schedule())

        def kept(name, shape, dtype):
            return keep.tile(shape, dtype, name=name, align_bytes=64)

        def rotating_bank(name, shape):
            return psum.tile(shape, F32, name=name, tag="rotating", bufs=ROTATING_BANKS)

        def score_bank(name, j, shape):
            return psum.tile(shape, F32, name=name, tag="score%d" % j, bufs=1)

        def half_cols(h):
            return slice(HALF * h, HALF * (h + 1))

        def tile_cols(i):
            return slice(P * i, P * (i + 1))

        def label(key):
            return "".join(str(part) for part in key)

        dosage = [("D", G) for G in range(4)]
        effect = [[("B", g, G) for G in range(4)] for g in range(2)]

        h_words = impute_words.bitcast(I32)
        h_scales = impute_scales.bitcast(I32)
        l_words = load_words[0].rearrange("p n t -> p (n t)").bitcast(I32)
        l_scales = load_scales[0].bitcast(I32)

        ident = kept("ident", [P, P], F32)
        x_raw = [kept("x_raw%d" % i, [P, 2, K], BF16) for i in range(2)]
        h_raw = [kept("h_raw%d" % G, [P, 2, GROUP // 2], I32) for G in range(4)]
        l_raw = [kept("l_raw%d" % G, [P, GROUP], I32) for G in range(4)]
        c_first = [kept("c_first%d" % h, [P, SLOTS, HALF], BF16) for h in range(2)]
        c_second = kept("c_second", [P, SLOTS, GROUP], BF16)
        hs_raw = kept("hs_raw", [P, 2, V // 4], I32)
        ls_raw = kept("ls_raw", [P, GROUP // 4], I32)
        factor_rows = kept("factor_rows", [8, GROUP], BF16)
        factor_sorted = kept("factor_sorted", [P, SLOTS, P], F32)
        factors = kept("factors", [P, 8, SLOTS], F32)
        slope_col = kept("slope_col", [P, 2, SLOTS], BF16)
        intercept_col = kept("intercept_col", [P, 2, SLOTS], BF16)
        scale_col = kept("scale_col", [P, 2, SLOTS], BF16)
        ancestry_all = kept("ancestry_all", [P, N], BF16)
        line_col = kept("line_col", [P, 2, 2 * SLOTS], F32)
        h_sorted = [kept("h_sorted%d" % G, [P, 2, 2 * GROUP], U8) for G in range(4)]
        hs_sorted = [kept("hs_sorted%d" % G, [P, 2, GROUP], U8) for G in range(4)]
        l_sorted = [kept("l_sorted%d" % G, [P, GROUP], I32) for G in range(4)]
        ls_sorted = kept("ls_sorted", [P, GROUP], U8)
        x_turned = kept("x_turned", [P, 2, N, 2], F32)
        x_codes = [kept("x_codes%d" % g, [P, N], I32) for g in range(2)]
        x_scales = [kept("x_scales%d" % g, [P, N], U8) for g in range(2)]
        c_codes = [kept("c_codes%d" % g, [P, GROUP], I32) for g in range(2)]
        c_scales = [kept("c_scales%d" % g, [P, GROUP], U8) for g in range(2)]
        codes = {}
        scales = {}
        for key in dosage:
            codes[key] = kept("codes%s" % label(key), [P, N], I32)
            scales[key] = kept("scales%s" % label(key), [P, N], U8)
        for key in effect[0] + effect[1]:
            codes[key] = [kept("codes%s_%d" % (label(key), h), [P, HALF], I32) for h in range(2)]
            scales[key] = [kept("scales%s_%d" % (label(key), h), [P, HALF], U8) for h in range(2)]
        y_turned = [kept("y_turned%d" % g, [P, SLOTS, N], F32) for g in range(2)]
        y_codes = [kept("y_codes%d" % g, [P, N], I32) for g in range(2)]
        y_scales = kept("y_scales", [P, 2, N], U8)

        make_identity(nc, ident[:])
        nc.vector.memset(factor_sorted[:, 0, :], 0.0)
        nc.vector.memset(ls_raw[:], 0)
        nc.vector.memset(hs_raw[:], 0)
        nc.scalar.activation(out=factor_sorted[:, 1:SLOTS, :],
                             in_=factor_sorted[:, 0:1, :].to_broadcast([P, SLOTS - 1, P]), func=ACT.Copy)

        def load_x(i):
            nc.sync.dma_start(out=x_raw[i][:], in_=x[2 * P * i:2 * P * (i + 1), :].rearrange("(i p) k -> p i k", p=P))

        def load_h(G):
            nc.sync.dma_start(out=h_raw[G][:], in_=h_words[:, :, half_cols(G)].rearrange("g p c -> p g c"))

        def load_l(G):
            nc.sync.dma_start(out=l_raw[G][:], in_=l_words[:, GROUP * G:GROUP * (G + 1)])

        def load_c(target, cols):
            nc.sync.dma_start(out=target[:], in_=trait_factors[:, cols].rearrange("(p f) c -> p f c", f=SLOTS))

        for first, vector in ((0, variant_weight), (4, dosage_scale)):
            nc.sync.dma_start(out=factor_rows[first:first + 4, :], in_=vector.rearrange("(G c) -> G c", G=4))
        load_c(c_first[0], half_cols(0))
        load_l(0)
        for Q in range(4):
            nc.sync.dma_start(out=ls_raw[32 * Q:32 * Q + 16, :],
                              in_=l_scales[4 * Q:4 * Q + 4, :].rearrange("r (G c) -> G r c", G=4))
        load_c(c_first[1], half_cols(1))
        load_l(1)
        load_x(0)
        load_x(1)
        for r in range(4):
            nc.sync.dma_start(out=hs_raw[r:P:32, :, :], in_=h_scales[:, r:16:4, :].rearrange("g Q c -> Q g c"))
        load_l(2)
        load_h(0)
        load_h(1)
        load_l(3)
        load_c(c_second, slice(GROUP, T))
        load_h(2)
        for column, vector in ((scale_col, trait_scale), (slope_col, slope), (intercept_col, intercept)):
            nc.sync.dma_start(out=column[:], in_=vector.rearrange("(g p j) -> p g j", g=2, j=SLOTS))
        load_h(3)
        nc.sync.dma_start(out=ancestry_all[:], in_=ancestry.partition_broadcast(P))

        def sort_h(G):
            nc.vector.tensor_copy(
                out=h_sorted[G][:].bitcast(I32).rearrange("p g (t q r) -> p g t q r", t=SLOTS, q=16),
                in_=h_raw[G][:].rearrange("p g (q t r) -> p g t q r", t=SLOTS, q=16))
            nc.vector.tensor_copy(
                out=hs_sorted[G][:].bitcast(I32).rearrange("p g (t q r) -> p g t q r", t=SLOTS, q=16),
                in_=hs_raw[:, :, tile_cols(G)].rearrange("p g (q t r) -> p g t q r", t=SLOTS, q=16))

        def sort_l(G):
            nc.vector.tensor_copy(
                out=l_sorted[G][:].rearrange("p (t q r) -> p t q r", t=SLOTS, q=16),
                in_=l_raw[G][:].rearrange("p (q t r) -> p t q r", t=SLOTS, q=16))

        def sort_l_scales():
            nc.vector.tensor_copy(
                out=ls_sorted[:].bitcast(I32).rearrange("p (t q r) -> p t q r", t=SLOTS, q=16),
                in_=ls_raw[:].rearrange("p (q t r) -> p t q r", t=SLOTS, q=16))

        def spread_factors():
            nc.vector.tensor_copy(out=factor_sorted[0:8, :, :].rearrange("p t (q r) -> p t q r", r=8),
                                  in_=factor_rows[:].rearrange("p (q t r) -> p t q r", t=SLOTS, r=8))
            bank = rotating_bank("factor_bank", [P, SLOTS, P])
            for t in range(SLOTS):
                nc.tensor.transpose(bank[:, t, :], factor_sorted[:, t, :], ident[:])
            nc.scalar.copy(out=factors[:], in_=bank[:, :, 0:8].rearrange("p t row -> p row t"))

        def turn_x(i):
            words = x_raw[i // 2][:, i % 2, :].bitcast(F32)
            bank = score_bank("x_bank%d" % i, i, [P, 2, 2, P])
            for g in range(2):
                for u in range(2):
                    nc.tensor.transpose(bank[:, g, u, :], words[:, HALF * g + u:HALF * (g + 1):2], ident[:])
            nc.scalar.copy(out=x_turned[:, :, tile_cols(i), :], in_=bank[:].rearrange("p g u n -> p g n u"))

        def quantize_x(g):
            nc.vector.quantize_mx(out=x_codes[g][:].bitcast(FP8X4), scales=x_scales[g][:],
                                  in_=x_turned[:, g, :, :].rearrange("p n u -> p (n u)").bitcast(BF16))

        grouped = {}

        def grouped_tile(key):
            if key not in grouped:
                if key in dosage[1:3]:
                    grouped[key] = flow.tile([P, GROUP, SLOTS], BF16, name="grouped_%s" % label(key),
                                             tag="handed_on", bufs=1, align_bytes=64)
                else:
                    grouped[key] = flow.tile([P, GROUP, SLOTS], BF16, name="grouped_%s" % label(key),
                                             tag="grouped", bufs=GROUPED_TILES, align_bytes=64)
            return grouped[key]

        def quantize(key, h, out_codes, out_scales):
            nc.vector.quantize_mx(out=out_codes.bitcast(FP8X4), scales=out_scales,
                                  in_=grouped[key][:, half_cols(h), :].rearrange("p c t -> p (c t)"))

        def group_c_first(h):
            nc.vector.tensor_copy(
                out=grouped_tile(("C", 0))[:, half_cols(h), :].rearrange("p (j m) f -> p j m f", j=SLOTS),
                in_=c_first[h][:].rearrange("p f (m j) -> p j m f", j=SLOTS))

        def group_c_second(h):
            nc.scalar.copy(
                out=grouped_tile(("C", 1))[:, half_cols(h), :].rearrange("p (j m) f -> p j m f", j=2),
                in_=c_second[:].rearrange("p f (m j) -> p j m f", j=SLOTS)[:, 2 * h:2 * h + 2, :, :])

        def quantize_c(g, h):
            quantize(("C", g), h, c_codes[g][:, half_cols(h)], c_scales[g][:, half_cols(h)])

        staged = {}

        def staged_tile(key):
            if key not in staged:
                staged[key] = flow.tile([P, SLOTS, GROUP], BF16, name="staged_%s" % label(key),
                                        tag="staged", bufs=STAGED_TILES, align_bytes=64)
            return staged[key]

        def effect_matmul(out, g, G, t, cols):
            nc.tensor.matmul_mx(out=out, lhsT=l_sorted[G][:, tile_cols(t)].bitcast(FP8X4),
                                lhsT_scale=ls_sorted[4 * G:, tile_cols(t)],
                                rhs=c_codes[g][:, cols].bitcast(FP8X4), rhs_scale=c_scales[g][:, cols],
                                start=True, stop=True)

        def joined(ap):
            return ap.rearrange("p (j h m) -> p h j m", j=SLOTS, h=2)

        def stage_dosage(G, t):
            bank = rotating_bank("bank_D%d%d" % (G, t), [P, N])
            for g in range(2):
                nc.tensor.matmul_mx(out=bank[:], lhsT=h_sorted[G][:, g, half_cols(t)].bitcast(FP4X4),
                                    lhsT_scale=hs_sorted[G][:, g, tile_cols(t)],
                                    rhs=x_codes[g][:].bitcast(FP8X4), rhs_scale=x_scales[g][:],
                                    start=(g == 0), stop=(g == 1))
            nc.scalar.activation(out=staged_tile(dosage[G])[:, t, :], in_=bank[:], func=ACT.Copy,
                                 scale=factors[:, 4 + G, t:t + 1])

        def stage_effect(g, G, t):
            bank = rotating_bank("bank_B%d%d%d" % (g, G, t), [P, GROUP])
            effect_matmul(bank[:], g, G, t, slice(0, GROUP))
            out, in_ = staged_tile(effect[g][G])[:, t, :], bank[:]
            if g == 0:
                out, in_ = joined(out), in_.rearrange("p (h j m) -> p h j m", j=SLOTS, h=2)
            nc.scalar.activation(out=out, in_=in_, func=ACT.Copy, scale=factors[:, G, t:t + 1])

        def stage_effect_half(g, G, h):
            target = staged_tile(effect[g][G])
            for pair in range(2):
                bank = rotating_bank("bank_B%d%d_%d%d" % (g, G, h, pair), [P, 2, HALF])
                for u in range(2):
                    effect_matmul(bank[:, u, :], g, G, 2 * pair + u, half_cols(h))
                for u in range(2):
                    t = 2 * pair + u
                    if g == 0:
                        out, in_ = joined(target[:, t, :])[:, h, :, :], bank[:, u, :].rearrange("p (j m) -> p j m", j=SLOTS)
                    else:
                        out, in_ = target[:, t, half_cols(h)], bank[:, u, :]
                    nc.scalar.activation(out=out, in_=in_, func=ACT.Copy, scale=factors[:, G, t:t + 1])

        def direct_effect(g, G, c, bank):
            for t in range(SLOTS):
                effect_matmul(bank[:, t, :], g, G, t, tile_cols(c))
            target = grouped_tile(effect[g][G])
            if g == 0:
                pair = slice(2 * (c % 2), 2 * (c % 2) + 2)
                out = target[:].rearrange("p (j h m) t -> p h j m t", j=SLOTS, h=2)[:, c // 2, pair, :, :]
                in0 = bank[:].rearrange("p t (j m) -> p j m t", j=2)
                in1 = factors[:, G, :].unsqueeze(1).unsqueeze(1).to_broadcast([P, 2, P // 2, SLOTS])
            else:
                out = target[:, tile_cols(c), :]
                in0 = bank[:].rearrange("p t n -> p n t")
                in1 = factors[:, G, :].unsqueeze(1).to_broadcast([P, P, SLOTS])
            nc.vector.tensor_tensor(out=out, in0=in0, in1=in1, op=ALU.mult)

        def direct_in_rotation(g, G, c):
            direct_effect(g, G, c, rotating_bank("bank_B%d%d%d" % (g, G, c), [P, SLOTS, P]))

        def direct_in_score_bank(g, G, c, j):
            direct_effect(g, G, c, score_bank("bank_B%d%d%d" % (g, G, c), j, [P, SLOTS, P]))

        def interleave(copy, key, source, h):
            copy(out=grouped_tile(key)[:, half_cols(h), :].rearrange("p (c i) t -> p c t i", i=4),
                 in_=source[:, :, half_cols(h)].rearrange("p t (c i) -> p c t i", i=4))

        def regroup(key, h):
            interleave(nc.vector.tensor_copy, key, staged[key], h)

        def regroup_on_gpsimd(key, h):
            nc.gpsimd.tensor_scalar(out=grouped_tile(key)[:, half_cols(h), :],
                                    in0=staged[key][:, :, half_cols(h)].rearrange("p t c -> p c t"),
                                    scalar1=1.0, scalar2=0.0, op0=ALU.mult, op1=ALU.add)

        def quantize_half(key, h):
            if key in dosage:
                quantize(key, h, codes[key][:, half_cols(h)], scales[key][:, half_cols(h)])
            else:
                quantize(key, h, codes[key][h][:], scales[key][h][:])

        def quantize_group(key):
            for h in range(2):
                quantize_half(key, h)

        def finish_group(key):
            for h in range(2):
                regroup(key, h)
            quantize_group(key)

        score = {}

        def second_stage(g, G, j):
            if G == 0:
                score[g, j] = score_bank("score%d_%d" % (g, j), j, [P, N])
            key = effect[g][G]
            nc.tensor.matmul_mx(out=score[g, j][:], lhsT=codes[key][j // 2][:, tile_cols(j % 2)].bitcast(FP8X4),
                                lhsT_scale=scales[key][j // 2][:, tile_cols(j % 2)],
                                rhs=codes[dosage[G]][:].bitcast(FP8X4), rhs_scale=scales[dosage[G]][:],
                                start=(G == 0), stop=(G == 3))

        def scale_lines():
            for a, column in enumerate((slope_col, intercept_col)):
                nc.vector.tensor_tensor(out=line_col[:, a, :], in0=column[:].rearrange("p g j -> p (g j)"),
                                        in1=scale_col[:].rearrange("p g j -> p (g j)"), op=ALU.mult)

        term = {}

        def ancestry_term_on_gpsimd(g, j):
            c = SLOTS * g + j
            term[g, j] = flow.tile([P, N], F32, name="term%d%d" % (g, j), tag="term", bufs=GPSIMD_TERMS)
            nc.gpsimd.tensor_scalar(out=term[g, j][:], in0=ancestry_all[:], scalar1=line_col[:, 0, c:c + 1],
                                    scalar2=line_col[:, 1, c:c + 1], op0=ALU.mult, op1=ALU.add)

        def ancestry_term_on_scalar(g, j):
            c = SLOTS * g + j
            term[g, j] = kept("term%d%d" % (g, j), [P, N], F32)
            nc.scalar.activation(out=term[g, j][:], in_=ancestry_all[:], func=ACT.Identity,
                                 scale=line_col[:, 0, c:c + 1], bias=line_col[:, 1, c:c + 1])

        def adjust(g, j, cols):
            nc.vector.scalar_tensor_tensor(out=y_turned[g][:, j, cols], in0=score[g, j][:, cols],
                                           scalar=scale_col[:, g, j:j + 1], in1=term[g, j][:, cols],
                                           op0=ALU.mult, op1=ALU.subtract)

        def round_y(copy, g, h):
            interleave(copy, ("Y", g), y_turned[g], h)

        def store_codes(g):
            for h in range(2):
                quantize(("Y", g), h, y_codes[g][:, half_cols(h)], y_scales[:, g, half_cols(h)])
            nc.sync.dma_start(out=out_1[g].rearrange("p m t -> p (m t)").bitcast(I32), in_=y_codes[g][:])

        def store_rows(g, i):
            bank = rotating_bank("y_bank%d_%d" % (g, i), [P, SLOTS, P])
            for j in range(SLOTS):
                nc.tensor.transpose(bank[:, j, :], y_turned[g][:, j, tile_cols(i)], ident[:])
            rows = flow.tile([P, P, SLOTS], F32, name="y_rows%d_%d" % (g, i), tag="y_rows", bufs=ROW_TILES)
            nc.scalar.copy(out=rows[:], in_=bank[:].rearrange("n j p -> n p j"))
            nc.sync.dma_start(out=out_0[tile_cols(i), GROUP * g:GROUP * (g + 1)], in_=rows[:].rearrange("n p j -> n (p j)"))

        spread_factors()
        group_c_first(0)
        sort_l(0)
        quantize_c(0, 0)
        sort_l_scales()
        stage_effect_half(0, 0, 0)
        group_c_first(1)
        sort_l(1)
        quantize_c(0, 1)
        for c in range(2):
            direct_in_score_bank(0, 1, c, 2 + c)
        stage_effect_half(0, 0, 1)
        for c in range(2, 4):
            direct_in_rotation(0, 1, c)

        for i in range(4):
            turn_x(i)
        regroup(effect[0][0], 0)
        sort_l(2)
        regroup(effect[0][0], 1)
        sort_h(0)
        for t in range(SLOTS):
            stage_effect(0, 2, t)
        quantize_x(0)
        quantize_x(1)
        sort_h(1)
        quantize_group(effect[0][1])
        sort_l(3)
        quantize_group(effect[0][0])

        for t in range(SLOTS):
            stage_dosage(0, t)
        finish_group(effect[0][2])
        sort_h(2)
        for t in range(2):
            stage_dosage(1, t)
        finish_group(dosage[0])
        scale_lines()
        for j in range(GPSIMD_TERMS):
            ancestry_term_on_gpsimd(0, j)
        group_c_second(0)
        for t in range(2, SLOTS):
            stage_dosage(1, t)
        group_c_second(1)
        for c in range(4):
            direct_in_score_bank(0, 3, c, c)
        for t in range(SLOTS):
            stage_dosage(2, t)
        sort_h(3)
        quantize_group(effect[0][3])
        regroup(dosage[1], 0)
        for h in range(2):
            quantize_c(1, h)
        regroup(dosage[1], 1)
        for t in range(2):
            second_stage(0, 0, t)
            stage_dosage(3, t)
        ancestry_term_on_scalar(0, 3)
        quantize_group(dosage[1])
        for h in range(2):
            regroup_on_gpsimd(dosage[2], h)
        for c in range(2):
            direct_in_rotation(1, 0, c)
        for c in range(2, 4):
            stage_dosage(3, c)
            direct_in_rotation(1, 0, c)
        interleave(nc.scalar.copy, dosage[3], staged[dosage[3]], 0)
        for j in range(2, SLOTS):
            second_stage(0, 0, j)
        quantize_group(dosage[2])

        for t in range(SLOTS):
            stage_effect(1, 1, t)
            second_stage(0, 1, t)
        regroup(dosage[3], 1)
        quantize_group(dosage[3])
        quantize_group(effect[1][0])
        for j in range(SLOTS):
            second_stage(0, 2, j)
        regroup(effect[1][1], 0)
        ancestry_term_on_scalar(1, 3)
        stage_effect_half(1, 2, 0)
        for j in range(SLOTS):
            second_stage(0, 3, j)
        stage_effect_half(1, 3, 0)
        for j in range(SLOTS):
            adjust(0, j, slice(0, N))
            if j < GPSIMD_TERMS:
                ancestry_term_on_gpsimd(1, j)
        regroup(effect[1][1], 1)

        for G in range(2, 4):
            for j in range(2 * (G - 2), 2 * (G - 1)):
                second_stage(1, 0, j)
            stage_effect_half(1, G, 1)
        regroup(effect[1][2], 0)
        quantize_group(effect[1][1])
        regroup(effect[1][3], 0)
        for G in range(2, 4):
            quantize_half(effect[1][G], 0)
        for i in range(2):
            store_rows(0, i)
        round_y(nc.scalar.copy, 0, 0)
        for j in range(SLOTS):
            second_stage(1, 1, j)
        for i in range(2, 4):
            store_rows(0, i)
        for j in range(2):
            for G in range(2, 4):
                second_stage(1, G, j)
        for G in range(2, 4):
            regroup(effect[1][G], 1)
        for G in range(2, 4):
            quantize_half(effect[1][G], 1)
        round_y(nc.scalar.copy, 0, 1)
        for j in range(2):
            adjust(1, j, slice(0, N))
        for j in range(2, SLOTS):
            for G in range(2, 4):
                second_stage(1, G, j)

        for j in range(2, SLOTS):
            adjust(1, j, half_cols(0))
        store_codes(0)
        for j in range(2, SLOTS):
            adjust(1, j, half_cols(1))
        round_y(nc.vector.tensor_copy, 1, 0)
        for i in range(4):
            store_rows(1, i)
        round_y(nc.vector.tensor_copy, 1, 1)
        store_codes(1)
        for Q in range(4):
            nc.scalar.dma_start(out=out_2[:, 4 * Q:4 * Q + 4, :].rearrange("g r n -> r g n").bitcast(I32),
                                in_=y_scales[32 * Q:32 * Q + 4, :, :].bitcast(I32))
